import numpy as np
import ml_dtypes


def mxq(x, axis, fmt="e4m3"):
    dtype, down = {"e4m3": (ml_dtypes.float8_e4m3fn, 7), "e5m2": (ml_dtypes.float8_e5m2, 14)}[fmt]
    v = np.moveaxis(np.asarray(x, np.float32).astype(ml_dtypes.bfloat16).astype(np.float64), axis, -1)
    blocks = v.reshape(v.shape[:-1] + (-1, 32))
    amax = np.abs(blocks).max(-1, keepdims=True)
    byte = np.maximum(np.where(amax > 0, np.frexp(amax)[1] - 1 + 127, 0) - down, 1)
    scale = np.exp2(byte - 127.0)
    codes = (blocks / scale).astype(np.float32).astype(dtype).astype(np.float64)
    return np.moveaxis((codes * scale).reshape(v.shape), -1, axis)


WIDE = False


def mx_kscale(k):
    if not WIDE:
        return np.ones(k)
    levels = np.array([10, -10, 5, -5, 0])
    if k % 512:
        return np.exp2(np.random.permutation(np.resize(levels, k // 32))).repeat(32)
    a = np.empty((k // 512, 16))
    for p in range(k // 512):
        a[p, :8] = np.random.permutation(np.resize(levels, 8))
        for g in range(8):
            far = levels[np.abs(levels - a[p, g]) >= 10]
            a[p, g + 8] = far[np.random.randint(len(far))]
    return np.exp2(a.ravel()).repeat(32)


def f64(x):
    return np.asarray(x).astype(np.float64)


def striped(idx):
    return np.tile(np.asarray(idx).reshape(-1, 16).T, (8, 1)).astype(np.uint16)


def unstriped(offs):
    return offs[:16].T.reshape(-1).astype(np.int64)


E2M1 = np.array([0.0, 0.5, 1.0, 1.5, 2.0, 3.0, 4.0, 6.0, -0.0, -0.5, -1.0, -1.5, -2.0, -3.0, -4.0, -6.0])


def pack_weight(w, fmt):
    k, n = w.shape
    w = f64(np.asarray(w, np.float32).astype(ml_dtypes.bfloat16)).reshape(k // 32, 32, n)
    amax = np.abs(w).max(1)
    if fmt == "e4m3":
        byte = np.frexp(amax)[1] - 1 + 127 - 7
    else:
        mant, ex = np.frexp(amax / 6.0)
        byte = np.where(mant > 0.5, ex, ex - 1) + 127
    byte = np.clip(np.where(amax > 0, byte, 1), 1, 254)
    scaled = (w * np.exp2(127.0 - byte)[:, None, :]).reshape(k, n).astype(np.float32)
    by_word = np.ascontiguousarray(scaled.reshape(k // 512, 128, 4, n).transpose(0, 1, 3, 2))
    if fmt == "e4m3":
        words = by_word.astype(ml_dtypes.float8_e4m3fn).view(np.uint8)
    else:
        c = by_word.astype(ml_dtypes.float4_e2m1fn).view(np.uint8) & 0xF
        words = (c[..., 0::2] | (c[..., 1::2] << 4)).reshape(k // 512, 128, 2 * n)
    return np.ascontiguousarray(words), np.ascontiguousarray(byte.astype(np.uint8).reshape(k // 512, 16, n))


def unpack_weight(words, scales, fmt):
    g, _, n = scales.shape
    words = np.ascontiguousarray(words).reshape(g, 128, n, -1)
    if fmt == "e4m3":
        vals = words.view(ml_dtypes.float8_e4m3fn).astype(np.float64)
    else:
        nib = np.empty((g, 128, n, 4), np.uint8)
        nib[..., 0::2] = words & 0xF
        nib[..., 1::2] = words >> 4
        vals = E2M1[nib]
    vals = vals * np.repeat(np.exp2(scales.astype(np.float64) - 127.0), 8, axis=1)[..., None]
    return vals.transpose(0, 1, 3, 2).reshape(g * 512, n)


B, N, T, D, DV, NQ = 2, 512, 2048, 1024, 128, 256
PAGE = 16
CAP = 2.0


def setup_inputs():
    n = np.random.standard_normal
    pages = np.random.permutation(T // PAGE)[:B * N // PAGE]
    idx = (pages[:, None] * PAGE + np.arange(PAGE)[None, :]).reshape(-1)
    s = mx_kscale(D)[:, None]
    u = np.ones(T)
    u[idx] = mx_kscale(B * N)
    r = np.random.uniform(0.5, 2.0, T)
    qp = [pack_weight(x, "e4m3") for x in n((B, D, NQ)) * s * (0.80 / np.sqrt(D))]
    k = n((D, T)) / s
    v = n((DV, T)) / (u * r)
    kp = pack_weight(k, "e4m3")
    return {
        "q_words": np.stack([x[0] for x in qp]),
        "q_scales": np.stack([x[1] for x in qp]),
        "k_words": kp[0],
        "k_scales": kp[1],
        "vT": v.astype(np.float32),
        "vs": np.tile(u * r, (128, 1)).astype(np.float32),
        "og": n((B, NQ, DV)).astype(np.float32),
        "offs": striped(idx),
    }


def reference(q_words, q_scales, k_words, k_scales, vT, vs, og, offs):
    idx = unstriped(offs)
    k = unpack_weight(k_words, k_scales, "e4m3")
    v = f64(vT)
    pick = lambda x: x[:, idx].reshape(x.shape[0], B, N).transpose(1, 0, 2)
    q = np.stack([unpack_weight(q_words[b], q_scales[b], "e4m3") for b in range(B)])
    score = q.transpose(0, 2, 1) @ pick(k)
    score = CAP * np.tanh(score / CAP)
    m = score.max(-1, keepdims=True)
    p = np.exp(score - m)
    total = p.sum(-1, keepdims=True)
    w = p * pick(f64(vs))[:, :1, :]
    y = mxq(w, 2, "e4m3") @ mxq(pick(v).transpose(0, 2, 1), 1, "e4m3")
    y = y / total
    y = y / (1.0 + np.exp(-f64(og)))
    return y

@@ -1,0 +1,266 @@
+from contextlib import ExitStack
+
+import concourse.mybir as mybir
+from concourse.masks import make_identity
+
+B, N, T, D, DV, NQ = 2, 512, 2048, 1024, 128, 256
+CAP = 2.0
+FLOPS = 2 * B * NQ * N * (D + DV)
+
+F32 = mybir.dt.float32
+BF16 = mybir.dt.bfloat16
+I32 = mybir.dt.int32
+U32 = mybir.dt.uint32
+U16 = mybir.dt.uint16
+U8 = mybir.dt.uint8
+FP8X4 = mybir.dt.float8_e4m3fn_x4
+ALU = mybir.AluOpType
+ACT = mybir.ActivationFunctionType
+
+P = 128
+PACK = 4
+PASSES = D // (P * PACK)
+QBLOCKS = NQ // P
+LIST_COLS = N // 16
+
+
+def tile_attend_soft_cap_gate_pgb2q256n512t2048_kernel(
+    tc, q_words, q_scales, k_words, k_scales, vT, vs, og, offs, out
+):
+    nc = tc.nc
+    with ExitStack() as ctx:
+        keep = ctx.enter_context(tc.tile_pool(name="keep", bufs=1))
+        late = ctx.enter_context(tc.tile_pool(name="late", bufs=1))
+        score_ps = ctx.enter_context(tc.psum_pool(name="score_ps", bufs=4))
+        turn_ps = ctx.enter_context(tc.psum_pool(name="turn_ps", bufs=4))
+
+        offsets = keep.tile([P, B * LIST_COLS], U16, name="offsets")
+        nc.sync.dma_start(offsets[:], offs)
+
+        def list_of(b):
+            return offsets[:, b * LIST_COLS : (b + 1) * LIST_COLS]
+
+        qs = keep.tile([P, B * PASSES, NQ], U8, name="qs", align_bytes=64)
+        ks_pool = late.tile([P, T], U8, name="ks_pool", offset=1024, align_bytes=64)
+        vs_pool = late.tile([P, T], F32, name="vs_pool", offset=10240, align_bytes=64)
+        nc.vector.memset(ks_pool[:].bitcast(I32), 0)
+        nc.gpsimd.memset(qs[:].rearrange("p a n -> p (a n)").bitcast(I32), 0)
+        nc.vector.memset(vs_pool[:, : T // 2 - 1], 0.0)
+        nc.vector.memset(vs_pool[:, T // 2 - 1 :], 0.0)
+
+        for quad in range(4):
+            nc.scalar.dma_start(
+                ks_pool[32 * quad : 32 * quad + 4 * PASSES, :].bitcast(I32),
+                k_scales[:, 4 * quad : 4 * quad + 4, :].bitcast(I32),
+            )
+        kw_pool = [keep.tile([P, T], U32, name="kw_pool%d" % o) for o in range(PASSES)]
+        qw = [
+            keep.tile([P, B, NQ], U32, name="qw0", align_bytes=64),
+            late.tile([P, B, NQ], U32, name="qw1", offset=0, align_bytes=64),
+        ]
+        v_pool = late.tile([P, T], F32, name="v_pool", offset=2048, align_bytes=64)
+        gate_in = late.tile([P, B * QBLOCKS, DV], F32, name="gate_in", offset=10240, align_bytes=64)
+
+        def load_keys(o):
+            nc.sync.dma_start(
+                kw_pool[o][:].bitcast(I32), k_words[o].rearrange("g t r -> g (t r)").bitcast(I32)
+            )
+
+        def load_queries(o):
+            nc.sync.dma_start(
+                qw[o][:].bitcast(I32), q_words[:, o].rearrange("b g q r -> g b (q r)").bitcast(I32)
+            )
+
+        load_keys(0)
+        load_queries(0)
+        load_keys(1)
+
+        q_scale_rows = q_scales.rearrange("b o f n -> f (b o) n")
+        for quad in range(4):
+            nc.gpsimd.dma_start(
+                qs[32 * quad : 32 * quad + 4, :, :].bitcast(I32),
+                q_scale_rows[4 * quad : 4 * quad + 4].bitcast(I32),
+            )
+        nc.scalar.dma_start(vs_pool[0:1, :], vs[0:1, :])
+        ident = keep.tile([P, P], F32, name="ident")
+        make_identity(nc, ident[:])
+
+        ks = keep.tile([P, B * N], U8, name="ks", align_bytes=64)
+        nc.vector.tensor_copy(ks[:], ks_pool[:].indirect(offsets[:]))
+        load_queries(1)
+        nc.sync.dma_start(v_pool[:], vT)
+
+        kw = {}
+
+        def gather_keys(o, b):
+            kw[o, b] = keep.tile([P, N], U32, name="kw%d%d" % (o, b), align_bytes=64)
+            nc.vector.tensor_copy(kw[o, b][:], kw_pool[o][:].indirect(list_of(b)))
+
+        blocks = [(b, j) for b in range(B) for j in range(QBLOCKS)]
+        scores = {}
+
+        def score_pass(o, b, j):
+            if o == 0:
+                scores[b, j] = score_ps.tile([P, N], F32, name="score", tag="acc")
+            cols = slice(j * P, (j + 1) * P)
+            nc.tensor.matmul_mx(
+                out=scores[b, j][:],
+                lhsT=qw[o][:, b, cols].bitcast(FP8X4),
+                lhsT_scale=qs[:, b * PASSES + o, cols],
+                rhs=kw[o, b][:].bitcast(FP8X4),
+                rhs_scale=ks[4 * o : P, b * N : (b + 1) * N],
+                start=(o == 0),
+                stop=(o == PASSES - 1),
+            )
+
+        for b in range(B):
+            gather_keys(0, b)
+            for j in range(QBLOCKS):
+                score_pass(0, b, j)
+
+        vs_row = keep.tile([P, B * N], F32, name="vs_row")
+        nc.vector.tensor_copy(vs_row[:], vs_pool[:].indirect(offsets[:]))
+        nc.sync.dma_start(gate_in[:], og.rearrange("b (j q) e -> q (b j) e", q=P))
+        vs_col = []
+        for b in range(B):
+            bank = turn_ps.tile([P, PACK, P], F32, name="vs_turned", tag="turn")
+            for t in range(PACK):
+                nc.tensor.transpose(bank[:, t, :], vs_row[:, b * N + t : (b + 1) * N : PACK], ident[:])
+            col = keep.tile([P, PACK], F32, name="vs_col%d" % b)
+            nc.scalar.activation(col[:], bank[:, :, 0], ACT.Copy)
+            vs_col.append(col)
+
+        for b in range(B):
+            gather_keys(1, b)
+            for j in range(QBLOCKS):
+                score_pass(1, b, j)
+
+        capped, neg_c, neg_m, prob, total = {}, {}, {}, {}, {}
+
+        def cap(i):
+            capped[i] = keep.tile([P, PACK, P], F32, name="capped%d" % i)
+            nc.scalar.activation(
+                capped[i][:],
+                scores[blocks[i]][:].rearrange("q (p t) -> q t p", t=PACK),
+                ACT.Tanh,
+                scale=1.0 / CAP,
+            )
+
+        def row_max(i):
+            neg_c[i] = keep.tile([P, N], F32, name="neg_c%d" % i)
+            neg_m[i] = keep.tile([P, 1], F32, name="neg_m%d" % i)
+            nc.vector.tensor_scalar(
+                neg_c[i][:],
+                capped[i][:].rearrange("q t p -> q (t p)"),
+                -CAP,
+                None,
+                ALU.mult,
+                ALU.min,
+                accum_out=neg_m[i][:],
+            )
+
+        def exponent(i):
+            prob[i] = keep.tile([P, N], F32, name="prob%d" % i)
+            total[i] = keep.tile([P, 1], F32, name="total%d" % i)
+            nc.scalar.activation(
+                prob[i][:], neg_c[i][:], ACT.Exp, bias=neg_m[i][:], scale=-1.0, accum_out=total[i][:]
+            )
+
+        w_bf, w_codes, w_scales, inv = {}, {}, {}, {}
+
+        def weigh(i):
+            b = blocks[i][0]
+            bank = turn_ps.tile([P, PACK, P], F32, name="p_turned", tag="turn")
+            for t in range(PACK):
+                nc.tensor.transpose(bank[:, t, :], prob[i][:, t * P : (t + 1) * P], ident[:])
+            w_bf[i] = keep.tile([P, P, PACK], BF16, name="w_bf%d" % i, align_bytes=64)
+            nc.vector.tensor_tensor(
+                w_bf[i][:],
+                bank[:].rearrange("p t q -> p q t"),
+                vs_col[b][:].unsqueeze(1).to_broadcast([P, P, PACK]),
+                ALU.mult,
+            )
+            inv[i] = keep.tile([P, 1], F32, name="inv%d" % i)
+            nc.vector.reciprocal(inv[i][:], total[i][:])
+
+        def quantise_w(i):
+            w_codes[i] = keep.tile([P, P], U32, name="w_codes%d" % i, align_bytes=64)
+            w_scales[i] = keep.tile([P, P], U8, name="w_scales%d" % i, align_bytes=64)
+            nc.vector.quantize_mx(
+                out=w_codes[i][:].bitcast(FP8X4),
+                scales=w_scales[i][:],
+                in_=w_bf[i][:].rearrange("p q t -> p (q t)"),
+            )
+
+        v_bf, v_codes, v_scales = {}, {}, {}
+
+        def turn_values(b):
+            picked = keep.tile([P, N], F32, name="v_picked%d" % b)
+            nc.vector.tensor_copy(picked[:], v_pool[:].indirect(list_of(b)))
+            bank = turn_ps.tile([P, PACK, DV], F32, name="v_turned", tag="turn")
+            for t in range(PACK):
+                nc.tensor.transpose(bank[:, t, :], picked[:, t:N:PACK], ident[:])
+            v_bf[b] = keep.tile([P, DV, PACK], BF16, name="v_bf%d" % b, align_bytes=64)
+            nc.scalar.copy(v_bf[b][:], bank[:].rearrange("p t e -> p e t"))
+
+        def quantise_v(b):
+            v_codes[b] = keep.tile([P, DV], U32, name="v_codes%d" % b, align_bytes=64)
+            v_scales[b] = keep.tile([P, DV], U8, name="v_scales%d" % b, align_bytes=64)
+            nc.vector.quantize_mx(
+                out=v_codes[b][:].bitcast(FP8X4),
+                scales=v_scales[b][:],
+                in_=v_bf[b][:].rearrange("p e t -> p (e t)"),
+            )
+
+        gate_tanh = keep.tile([P, B * QBLOCKS, DV], F32, name="gate_tanh")
+        gate = keep.tile([P, B * QBLOCKS, DV], F32, name="gate")
+
+        def make_gate():
+            nc.scalar.activation(gate_tanh[:], gate_in[:], ACT.Tanh, scale=0.5)
+            nc.scalar.activation(gate[:], gate_tanh[:], ACT.Copy, bias=0.5, scale=0.5)
+
+        def finish(i):
+            b, j = blocks[i]
+            y = score_ps.tile([P, DV], F32, name="y", tag="acc")
+            nc.tensor.matmul_mx(
+                out=y[:],
+                lhsT=w_codes[i][:].bitcast(FP8X4),
+                lhsT_scale=w_scales[i][:],
+                rhs=v_codes[b][:].bitcast(FP8X4),
+                rhs_scale=v_scales[b][:],
+                start=True,
+                stop=True,
+            )
+            res = keep.tile([P, DV], F32, name="res%d" % i)
+            nc.vector.scalar_tensor_tensor(res[:], y[:], inv[i][:], gate[:, i, :], ALU.mult, ALU.mult)
+            nc.sync.dma_start(out[b, j * P : (j + 1) * P, :], res[:])
+
+        cap(0)
+        row_max(0)
+        cap(1)
+        exponent(0)
+        row_max(1)
+        cap(2)
+        exponent(1)
+        row_max(2)
+        cap(3)
+        weigh(0)
+        exponent(2)
+        row_max(3)
+        turn_values(0)
+        weigh(1)
+        exponent(3)
+        quantise_w(0)
+        quantise_v(0)
+        make_gate()
+        turn_values(1)
+        quantise_w(1)
+        weigh(2)
+        finish(0)
+        weigh(3)
+        quantise_v(1)
+        finish(1)
+        quantise_w(2)
+        quantise_w(3)
+        finish(2)
+        finish(3)

@@ -1,7 +1,6 @@
 from contextlib import ExitStack
 
 import concourse.mybir as mybir
-from concourse.masks import make_identity
 
 B, N, T, D, DV, NQ = 2, 512, 2048, 1024, 128, 256
 CAP = 2.0
@@ -44,18 +43,13 @@ def tile_attend_soft_cap_gate_pgb2q256n512t2048_kernel(
         ks_pool = late.tile([P, T], U8, name="ks_pool", offset=1024, align_bytes=64)
         vs_pool = late.tile([P, T], F32, name="vs_pool", offset=10240, align_bytes=64)
         nc.vector.memset(ks_pool[:].bitcast(I32), 0)
-        nc.gpsimd.memset(qs[:].rearrange("p a n -> p (a n)").bitcast(I32), 0)
-        nc.vector.memset(vs_pool[:, : T // 2 - 1], 0.0)
-        nc.vector.memset(vs_pool[:, T // 2 - 1 :], 0.0)
+        nc.vector.memset(vs_pool[:, : T - 256], 0.0)
+        nc.gpsimd.memset(vs_pool[:, T - 256 :], 0.0)
+        nc.vector.memset(qs[:].rearrange("p a n -> p (a n)").bitcast(I32), 0)
 
-        for quad in range(4):
-            nc.scalar.dma_start(
-                ks_pool[32 * quad : 32 * quad + 4 * PASSES, :].bitcast(I32),
-                k_scales[:, 4 * quad : 4 * quad + 4, :].bitcast(I32),
-            )
-        kw_pool = [keep.tile([P, T], U32, name="kw_pool%d" % o) for o in range(PASSES)]
+        kw_pool = late.tile([P, PASSES, T], U32, name="kw_pool", offset=20480, align_bytes=64)
         qw = [
-            keep.tile([P, B, NQ], U32, name="qw0", align_bytes=64),
+            late.tile([P, B, NQ], U32, name="qw0", offset=36864, align_bytes=64),
             late.tile([P, B, NQ], U32, name="qw1", offset=0, align_bytes=64),
         ]
         v_pool = late.tile([P, T], F32, name="v_pool", offset=2048, align_bytes=64)
@@ -63,7 +57,7 @@ def tile_attend_soft_cap_gate_pgb2q256n512t2048_kernel(
 
         def load_keys(o):
             nc.sync.dma_start(
-                kw_pool[o][:].bitcast(I32), k_words[o].rearrange("g t r -> g (t r)").bitcast(I32)
+                kw_pool[:, o, :].bitcast(I32), k_words[o].rearrange("g t r -> g (t r)").bitcast(I32)
             )
 
         def load_queries(o):
@@ -71,19 +65,34 @@ def tile_attend_soft_cap_gate_pgb2q256n512t2048_kernel(
                 qw[o][:].bitcast(I32), q_words[:, o].rearrange("b g q r -> g b (q r)").bitcast(I32)
             )
 
+        for quad in range(4):
+            nc.sync.dma_start(
+                ks_pool[32 * quad : 32 * quad + 4 * PASSES, :].bitcast(I32),
+                k_scales[:, 4 * quad : 4 * quad + 4, :].bitcast(I32),
+            )
+        zeros = late.tile([P, P], F32, name="zeros", offset=36864 - 256, align_bytes=64)
+        ident = keep.tile([P, P], F32, name="ident")
+        nc.gpsimd.memset(zeros[:], 0.0)
+        nc.gpsimd.affine_select(
+            out=ident[:],
+            in_=zeros[:],
+            compare_op=ALU.not_equal,
+            fill=1.0,
+            base=0,
+            pattern=[[-1, P]],
+            channel_multiplier=1,
+        )
         load_keys(0)
         load_queries(0)
         load_keys(1)
+        nc.scalar.dma_start(vs_pool[0:1, :], vs[0:1, :])
 
         q_scale_rows = q_scales.rearrange("b o f n -> f (b o) n")
         for quad in range(4):
-            nc.gpsimd.dma_start(
+            nc.scalar.dma_start(
                 qs[32 * quad : 32 * quad + 4, :, :].bitcast(I32),
                 q_scale_rows[4 * quad : 4 * quad + 4].bitcast(I32),
             )
-        nc.scalar.dma_start(vs_pool[0:1, :], vs[0:1, :])
-        ident = keep.tile([P, P], F32, name="ident")
-        make_identity(nc, ident[:])
 
         ks = keep.tile([P, B * N], U8, name="ks", align_bytes=64)
         nc.vector.tensor_copy(ks[:], ks_pool[:].indirect(offsets[:]))
@@ -93,8 +102,13 @@ def tile_attend_soft_cap_gate_pgb2q256n512t2048_kernel(
         kw = {}
 
         def gather_keys(o, b):
-            kw[o, b] = keep.tile([P, N], U32, name="kw%d%d" % (o, b), align_bytes=64)
-            nc.vector.tensor_copy(kw[o, b][:], kw_pool[o][:].indirect(list_of(b)))
+            if o == 0:
+                kw[o, b] = keep.tile([P, N], U32, name="kw%d%d" % (o, b), align_bytes=64)
+            else:
+                kw[o, b] = late.tile(
+                    [P, N], U32, name="kw%d%d" % (o, b), offset=12288 + 2048 * b, align_bytes=64
+                )
+            nc.vector.tensor_copy(kw[o, b][:], kw_pool[:, o, :].indirect(list_of(b)))
 
         blocks = [(b, j) for b in range(B) for j in range(QBLOCKS)]
         scores = {}

@@ -1,6 +1,7 @@
 from contextlib import ExitStack
 
 import concourse.mybir as mybir
+from concourse.masks import make_identity
 
 B, N, T, D, DV, NQ = 2, 512, 2048, 1024, 128, 256
 CAP = 2.0
@@ -40,29 +41,33 @@ def tile_attend_soft_cap_gate_pgb2q256n512t2048_kernel(
             return offsets[:, b * LIST_COLS : (b + 1) * LIST_COLS]
 
         qs = keep.tile([P, B * PASSES, NQ], U8, name="qs", align_bytes=64)
-        ks_pool = late.tile([P, T], U8, name="ks_pool", offset=1024, align_bytes=64)
-        vs_pool = late.tile([P, T], F32, name="vs_pool", offset=10240, align_bytes=64)
+        ks_pool = late.tile([P, T], U8, name="ks_pool", offset=3072, align_bytes=64)
+        vs_pool = late.tile([P, T], F32, name="vs_pool", offset=12288, align_bytes=64)
+        zeros = late.tile([P, NQ // 4], I32, name="zeros", offset=28672 - 128, align_bytes=64)
+        ident = keep.tile([P, P], F32, name="ident")
+        nc.vector.memset(zeros[:], 0)
         nc.vector.memset(ks_pool[:].bitcast(I32), 0)
-        nc.vector.memset(vs_pool[:, : T - 256], 0.0)
-        nc.gpsimd.memset(vs_pool[:, T - 256 :], 0.0)
-        nc.vector.memset(qs[:].rearrange("p a n -> p (a n)").bitcast(I32), 0)
+        nc.vector.tensor_copy(qs[:, 0, :].bitcast(I32), zeros[:])
+        nc.vector.memset(vs_pool[:], 0.0)
+        nc.vector.memset(qs[:, 1:, :].rearrange("p a n -> p (a n)").bitcast(I32), 0)
+        make_identity(nc, ident[:])
 
-        kw_pool = late.tile([P, PASSES, T], U32, name="kw_pool", offset=20480, align_bytes=64)
-        qw = [
-            late.tile([P, B, NQ], U32, name="qw0", offset=36864, align_bytes=64),
-            late.tile([P, B, NQ], U32, name="qw1", offset=0, align_bytes=64),
+        kw_pool = [
+            late.tile([P, T], U32, name="kw_pool0", offset=20480, align_bytes=64),
+            late.tile([P, T], U32, name="kw_pool1", offset=4096, align_bytes=64),
         ]
-        v_pool = late.tile([P, T], F32, name="v_pool", offset=2048, align_bytes=64)
-        gate_in = late.tile([P, B * QBLOCKS, DV], F32, name="gate_in", offset=10240, align_bytes=64)
+        qw = late.tile([P, B, PASSES, NQ], U32, name="qw", offset=0, align_bytes=64)
+        v_pool = late.tile([P, T], F32, name="v_pool", offset=28672, align_bytes=64)
+        gate_in = late.tile([P, B * QBLOCKS, DV], F32, name="gate_in", offset=12288, align_bytes=64)
 
         def load_keys(o):
             nc.sync.dma_start(
-                kw_pool[:, o, :].bitcast(I32), k_words[o].rearrange("g t r -> g (t r)").bitcast(I32)
+                kw_pool[o][:].bitcast(I32), k_words[o].rearrange("g t r -> g (t r)").bitcast(I32)
             )
 
-        def load_queries(o):
+        def load_queries(b):
             nc.sync.dma_start(
-                qw[o][:].bitcast(I32), q_words[:, o].rearrange("b g q r -> g b (q r)").bitcast(I32)
+                qw[:, b].bitcast(I32), q_words[b].rearrange("o g q r -> g o (q r)").bitcast(I32)
             )
 
         for quad in range(4):
@@ -70,23 +75,9 @@ def tile_attend_soft_cap_gate_pgb2q256n512t2048_kernel(
                 ks_pool[32 * quad : 32 * quad + 4 * PASSES, :].bitcast(I32),
                 k_scales[:, 4 * quad : 4 * quad + 4, :].bitcast(I32),
             )
-        zeros = late.tile([P, P], F32, name="zeros", offset=36864 - 256, align_bytes=64)
-        ident = keep.tile([P, P], F32, name="ident")
-        nc.gpsimd.memset(zeros[:], 0.0)
-        nc.gpsimd.affine_select(
-            out=ident[:],
-            in_=zeros[:],
-            compare_op=ALU.not_equal,
-            fill=1.0,
-            base=0,
-            pattern=[[-1, P]],
-            channel_multiplier=1,
-        )
+        nc.sync.dma_start(v_pool[:], vT)
         load_keys(0)
-        load_queries(0)
-        load_keys(1)
         nc.scalar.dma_start(vs_pool[0:1, :], vs[0:1, :])
-
         q_scale_rows = q_scales.rearrange("b o f n -> f (b o) n")
         for quad in range(4):
             nc.scalar.dma_start(
@@ -96,19 +87,21 @@ def tile_attend_soft_cap_gate_pgb2q256n512t2048_kernel(
 
         ks = keep.tile([P, B * N], U8, name="ks", align_bytes=64)
         nc.vector.tensor_copy(ks[:], ks_pool[:].indirect(offsets[:]))
+        load_keys(1)
+        load_queries(0)
         load_queries(1)
-        nc.sync.dma_start(v_pool[:], vT)
 
         kw = {}
 
-        def gather_keys(o, b):
-            if o == 0:
-                kw[o, b] = keep.tile([P, N], U32, name="kw%d%d" % (o, b), align_bytes=64)
-            else:
-                kw[o, b] = late.tile(
-                    [P, N], U32, name="kw%d%d" % (o, b), offset=12288 + 2048 * b, align_bytes=64
-                )
-            nc.vector.tensor_copy(kw[o, b][:], kw_pool[:, o, :].indirect(list_of(b)))
+        def gather_first_keys():
+            both = late.tile([P, B * N], U32, name="kw0", offset=14336, align_bytes=64)
+            nc.vector.tensor_copy(both[:], kw_pool[0][:].indirect(offsets[:]))
+            for b in range(B):
+                kw[0, b] = both[:, b * N : (b + 1) * N]
+
+        def gather_second_keys(b):
+            kw[1, b] = keep.tile([P, N], U32, name="kw1%d" % b, align_bytes=64)[:]
+            nc.vector.tensor_copy(kw[1, b], kw_pool[1][:].indirect(list_of(b)))
 
         blocks = [(b, j) for b in range(B) for j in range(QBLOCKS)]
         scores = {}
@@ -119,37 +112,17 @@ def tile_attend_soft_cap_gate_pgb2q256n512t2048_kernel(
             cols = slice(j * P, (j + 1) * P)
             nc.tensor.matmul_mx(
                 out=scores[b, j][:],
-                lhsT=qw[o][:, b, cols].bitcast(FP8X4),
+                lhsT=qw[:, b, o, cols].bitcast(FP8X4),
                 lhsT_scale=qs[:, b * PASSES + o, cols],
-                rhs=kw[o, b][:].bitcast(FP8X4),
+                rhs=kw[o, b].bitcast(FP8X4),
                 rhs_scale=ks[4 * o : P, b * N : (b + 1) * N],
                 start=(o == 0),
                 stop=(o == PASSES - 1),
             )
 
-        for b in range(B):
-            gather_keys(0, b)
-            for j in range(QBLOCKS):
-                score_pass(0, b, j)
-
-        vs_row = keep.tile([P, B * N], F32, name="vs_row")
-        nc.vector.tensor_copy(vs_row[:], vs_pool[:].indirect(offsets[:]))
-        nc.sync.dma_start(gate_in[:], og.rearrange("b (j q) e -> q (b j) e", q=P))
-        vs_col = []
-        for b in range(B):
-            bank = turn_ps.tile([P, PACK, P], F32, name="vs_turned", tag="turn")
-            for t in range(PACK):
-                nc.tensor.transpose(bank[:, t, :], vs_row[:, b * N + t : (b + 1) * N : PACK], ident[:])
-            col = keep.tile([P, PACK], F32, name="vs_col%d" % b)
-            nc.scalar.activation(col[:], bank[:, :, 0], ACT.Copy)
-            vs_col.append(col)
-
-        for b in range(B):
-            gather_keys(1, b)
-            for j in range(QBLOCKS):
-                score_pass(1, b, j)
-
-        capped, neg_c, neg_m, prob, total = {}, {}, {}, {}, {}
+        capped, neg_c, neg_m, prob = {}, {}, {}, {}
+        total = keep.tile([P, B * QBLOCKS], F32, name="total")
+        inv = keep.tile([P, B * QBLOCKS], F32, name="inv")
 
         def cap(i):
             capped[i] = keep.tile([P, PACK, P], F32, name="capped%d" % i)
@@ -175,12 +148,11 @@ def tile_attend_soft_cap_gate_pgb2q256n512t2048_kernel(
 
         def exponent(i):
             prob[i] = keep.tile([P, N], F32, name="prob%d" % i)
-            total[i] = keep.tile([P, 1], F32, name="total%d" % i)
             nc.scalar.activation(
-                prob[i][:], neg_c[i][:], ACT.Exp, bias=neg_m[i][:], scale=-1.0, accum_out=total[i][:]
+                prob[i][:], neg_c[i][:], ACT.Exp, bias=neg_m[i][:], scale=-1.0, accum_out=total[:, i : i + 1]
             )
 
-        w_bf, w_codes, w_scales, inv = {}, {}, {}, {}
+        w_bf, w_codes, w_scales = {}, {}, {}
 
         def weigh(i):
             b = blocks[i][0]
@@ -194,8 +166,10 @@ def tile_attend_soft_cap_gate_pgb2q256n512t2048_kernel(
                 vs_col[b][:].unsqueeze(1).to_broadcast([P, P, PACK]),
                 ALU.mult,
             )
-            inv[i] = keep.tile([P, 1], F32, name="inv%d" % i)
-            nc.vector.reciprocal(inv[i][:], total[i][:])
+
+        def invert(b):
+            cols = slice(b * QBLOCKS, (b + 1) * QBLOCKS)
+            nc.vector.reciprocal(inv[:, cols], total[:, cols])
 
         def quantise_w(i):
             w_codes[i] = keep.tile([P, P], U32, name="w_codes%d" % i, align_bytes=64)
@@ -206,24 +180,29 @@ def tile_attend_soft_cap_gate_pgb2q256n512t2048_kernel(
                 in_=w_bf[i][:].rearrange("p q t -> p (q t)"),
             )
 
-        v_bf, v_codes, v_scales = {}, {}, {}
+        v_bf = keep.tile([P, B, DV, PACK], BF16, name="v_bf", align_bytes=64)
+        v_codes = keep.tile([P, B, DV], U32, name="v_codes", align_bytes=64)
+        v_scales = keep.tile([P, B, DV], U8, name="v_scales", align_bytes=64)
 
         def turn_values(b):
-            picked = keep.tile([P, N], F32, name="v_picked%d" % b)
-            nc.vector.tensor_copy(picked[:], v_pool[:].indirect(list_of(b)))
-            bank = turn_ps.tile([P, PACK, DV], F32, name="v_turned", tag="turn")
-            for t in range(PACK):
-                nc.tensor.transpose(bank[:, t, :], picked[:, t:N:PACK], ident[:])
-            v_bf[b] = keep.tile([P, DV, PACK], BF16, name="v_bf%d" % b, align_bytes=64)
-            nc.scalar.copy(v_bf[b][:], bank[:].rearrange("p t e -> p e t"))
+            picked = keep.tile([P, 2, P, 2], BF16, name="v_picked%d" % b)
+            nc.scalar.activation(
+                picked[:].rearrange("e u p h -> e p u h"), v_half[:].indirect(list_of(b)), ACT.Copy
+            )
+            words = picked[:].rearrange("e u p h -> e (u p h)").bitcast(F32)
+            bank = turn_ps.tile([P, 2, DV], F32, name="v_turned", tag="turn")
+            for u in range(2):
+                nc.tensor.transpose(bank[:, u, :], words[:, u * P : (u + 1) * P], ident[:])
+            nc.scalar.copy(
+                v_bf[:, b].rearrange("p e t -> p (e t)").bitcast(F32).rearrange("p (e u) -> p e u", u=2),
+                bank[:].rearrange("p u e -> p e u"),
+            )
 
-        def quantise_v(b):
-            v_codes[b] = keep.tile([P, DV], U32, name="v_codes%d" % b, align_bytes=64)
-            v_scales[b] = keep.tile([P, DV], U8, name="v_scales%d" % b, align_bytes=64)
+        def quantise_v():
             nc.vector.quantize_mx(
-                out=v_codes[b][:].bitcast(FP8X4),
-                scales=v_scales[b][:],
-                in_=v_bf[b][:].rearrange("p e t -> p (e t)"),
+                out=v_codes[:].rearrange("p b e -> p (b e)").bitcast(FP8X4),
+                scales=v_scales[:].rearrange("p b e -> p (b e)"),
+                in_=v_bf[:].rearrange("p b e t -> p (b e t)"),
             )
 
         gate_tanh = keep.tile([P, B * QBLOCKS, DV], F32, name="gate_tanh")
@@ -231,7 +210,7 @@ def tile_attend_soft_cap_gate_pgb2q256n512t2048_kernel(
 
         def make_gate():
             nc.scalar.activation(gate_tanh[:], gate_in[:], ACT.Tanh, scale=0.5)
-            nc.scalar.activation(gate[:], gate_tanh[:], ACT.Copy, bias=0.5, scale=0.5)
+            nc.gpsimd.tensor_scalar(gate[:], gate_tanh[:], 0.5, 0.5, ALU.mult, ALU.add)
 
         def finish(i):
             b, j = blocks[i]
@@ -240,41 +219,66 @@ def tile_attend_soft_cap_gate_pgb2q256n512t2048_kernel(
                 out=y[:],
                 lhsT=w_codes[i][:].bitcast(FP8X4),
                 lhsT_scale=w_scales[i][:],
-                rhs=v_codes[b][:].bitcast(FP8X4),
-                rhs_scale=v_scales[b][:],
+                rhs=v_codes[:, b, :].bitcast(FP8X4),
+                rhs_scale=v_scales[:, b, :],
                 start=True,
                 stop=True,
             )
             res = keep.tile([P, DV], F32, name="res%d" % i)
-            nc.vector.scalar_tensor_tensor(res[:], y[:], inv[i][:], gate[:, i, :], ALU.mult, ALU.mult)
+            nc.vector.scalar_tensor_tensor(res[:], y[:], inv[:, i : i + 1], gate[:, i, :], ALU.mult, ALU.mult)
             nc.sync.dma_start(out[b, j * P : (j + 1) * P, :], res[:])
 
+        vs_col = []
+
+        def turn_token_scales(b):
+            bank = turn_ps.tile([P, PACK, P], F32, name="vs_turned", tag="turn")
+            for t in range(PACK):
+                nc.tensor.transpose(bank[:, t, :], vs_row[:, b * N + t : (b + 1) * N : PACK], ident[:])
+            col = keep.tile([P, PACK], F32, name="vs_col%d" % b)
+            nc.scalar.activation(col[:], bank[:, :, 0], ACT.Copy)
+            vs_col.append(col)
+
+        vs_row = keep.tile([P, B * N], F32, name="vs_row")
+        nc.vector.tensor_copy(vs_row[:], vs_pool[:].indirect(offsets[:]))
+        nc.sync.dma_start(gate_in[:], og.rearrange("b (j q) e -> q (b j) e", q=P))
+        gather_first_keys()
+        v_half = keep.tile([P, T], BF16, name="v_half")
+        nc.scalar.activation(v_half[:], v_pool[:], ACT.Copy)
+        turn_values(0)
+        turn_values(1)
+        turn_token_scales(0)
+        turn_token_scales(1)
+        for b in range(B):
+            for j in range(QBLOCKS):
+                score_pass(0, b, j)
+            gather_second_keys(b)
+            for j in range(QBLOCKS):
+                score_pass(1, b, j)
         cap(0)
         row_max(0)
         cap(1)
+        make_gate()
         exponent(0)
         row_max(1)
         cap(2)
         exponent(1)
         row_max(2)
         cap(3)
-        weigh(0)
         exponent(2)
         row_max(3)
-        turn_values(0)
-        weigh(1)
+        weigh(0)
         exponent(3)
+        quantise_v()
+        weigh(1)
         quantise_w(0)
-        quantise_v(0)
-        make_gate()
-        turn_values(1)
-        quantise_w(1)
+        invert(0)
         weigh(2)
+        quantise_w(1)
         finish(0)
         weigh(3)
-        quantise_v(1)
-        finish(1)
         quantise_w(2)
+        finish(1)
+        invert(1)
         quantise_w(3)
         finish(2)
         finish(3)

@@ -41,33 +41,35 @@ def tile_attend_soft_cap_gate_pgb2q256n512t2048_kernel(
             return offsets[:, b * LIST_COLS : (b + 1) * LIST_COLS]
 
         qs = keep.tile([P, B * PASSES, NQ], U8, name="qs", align_bytes=64)
-        ks_pool = late.tile([P, T], U8, name="ks_pool", offset=3072, align_bytes=64)
-        vs_pool = late.tile([P, T], F32, name="vs_pool", offset=12288, align_bytes=64)
-        zeros = late.tile([P, NQ // 4], I32, name="zeros", offset=28672 - 128, align_bytes=64)
         ident = keep.tile([P, P], F32, name="ident")
-        nc.vector.memset(zeros[:], 0)
-        nc.vector.memset(ks_pool[:].bitcast(I32), 0)
-        nc.vector.tensor_copy(qs[:, 0, :].bitcast(I32), zeros[:])
-        nc.vector.memset(vs_pool[:], 0.0)
-        nc.vector.memset(qs[:, 1:, :].rearrange("p a n -> p (a n)").bitcast(I32), 0)
-        make_identity(nc, ident[:])
-
-        kw_pool = [
-            late.tile([P, T], U32, name="kw_pool0", offset=20480, align_bytes=64),
-            late.tile([P, T], U32, name="kw_pool1", offset=4096, align_bytes=64),
+        vs_pool = late.tile([P, T], F32, name="vs_pool", offset=0, align_bytes=64)
+        gate_in = late.tile([P, B * QBLOCKS, DV], F32, name="gate_in", offset=0, align_bytes=64)
+        v_pool = late.tile([P, T], F32, name="v_pool", offset=8192, align_bytes=64)
+        zero_words = late.tile([P, B * PASSES * NQ // 4], I32, name="zero_words", offset=16384 - 512, align_bytes=64)
+        kw_pool = late.tile([P, PASSES, T], U32, name="kw_pool", offset=16384, align_bytes=64)
+        ks_pool = late.tile([P, T], U8, name="ks_pool", offset=32768, align_bytes=64)
+        v_half = keep.tile([P, T], BF16, name="v_half")
+        qw = [
+            keep.tile([P, PASSES, NQ], U32, name="qw0", align_bytes=64),
+            late.tile([P, PASSES, NQ], U32, name="qw1", offset=32768, align_bytes=64),
         ]
-        qw = late.tile([P, B, PASSES, NQ], U32, name="qw", offset=0, align_bytes=64)
-        v_pool = late.tile([P, T], F32, name="v_pool", offset=28672, align_bytes=64)
-        gate_in = late.tile([P, B * QBLOCKS, DV], F32, name="gate_in", offset=12288, align_bytes=64)
+
+        nc.gpsimd.memset(ks_pool[:].bitcast(I32), 0)
+        nc.gpsimd.memset(vs_pool[:, :760], 0.0)
+        nc.gpsimd.memset(zero_words[:], 0)
+        nc.vector.memset(vs_pool[:, 760:1403], 0.0)
+        nc.vector.memset(vs_pool[:, 1403:], 0.0)
+        nc.vector.tensor_copy(qs[:].rearrange("p a n -> p (a n)").bitcast(I32), zero_words[:])
+        make_identity(nc, ident[:])
 
         def load_keys(o):
             nc.sync.dma_start(
-                kw_pool[o][:].bitcast(I32), k_words[o].rearrange("g t r -> g (t r)").bitcast(I32)
+                kw_pool[:, o, :].bitcast(I32), k_words[o].rearrange("g t r -> g (t r)").bitcast(I32)
             )
 
         def load_queries(b):
             nc.sync.dma_start(
-                qw[:, b].bitcast(I32), q_words[b].rearrange("o g q r -> g o (q r)").bitcast(I32)
+                qw[b][:].bitcast(I32), q_words[b].rearrange("o g q r -> g o (q r)").bitcast(I32)
             )
 
         for quad in range(4):
@@ -75,49 +77,49 @@ def tile_attend_soft_cap_gate_pgb2q256n512t2048_kernel(
                 ks_pool[32 * quad : 32 * quad + 4 * PASSES, :].bitcast(I32),
                 k_scales[:, 4 * quad : 4 * quad + 4, :].bitcast(I32),
             )
+        load_queries(0)
+        nc.sync.dma_start(vs_pool[0:1, :], vs[0:1, :])
         nc.sync.dma_start(v_pool[:], vT)
         load_keys(0)
-        nc.scalar.dma_start(vs_pool[0:1, :], vs[0:1, :])
+        load_keys(1)
         q_scale_rows = q_scales.rearrange("b o f n -> f (b o) n")
         for quad in range(4):
-            nc.scalar.dma_start(
+            nc.sync.dma_start(
                 qs[32 * quad : 32 * quad + 4, :, :].bitcast(I32),
                 q_scale_rows[4 * quad : 4 * quad + 4].bitcast(I32),
             )
 
         ks = keep.tile([P, B * N], U8, name="ks", align_bytes=64)
         nc.vector.tensor_copy(ks[:], ks_pool[:].indirect(offsets[:]))
-        load_keys(1)
-        load_queries(0)
         load_queries(1)
 
         kw = {}
 
         def gather_first_keys():
-            both = late.tile([P, B * N], U32, name="kw0", offset=14336, align_bytes=64)
-            nc.vector.tensor_copy(both[:], kw_pool[0][:].indirect(offsets[:]))
+            both = late.tile([P, B * N], U32, name="kw0", offset=2048, align_bytes=64)
+            nc.vector.tensor_copy(both[:], kw_pool[:, 0, :].indirect(offsets[:]))
             for b in range(B):
                 kw[0, b] = both[:, b * N : (b + 1) * N]
 
         def gather_second_keys(b):
             kw[1, b] = keep.tile([P, N], U32, name="kw1%d" % b, align_bytes=64)[:]
-            nc.vector.tensor_copy(kw[1, b], kw_pool[1][:].indirect(list_of(b)))
+            nc.vector.tensor_copy(kw[1, b], kw_pool[:, 1, :].indirect(list_of(b)))
 
         blocks = [(b, j) for b in range(B) for j in range(QBLOCKS)]
         scores = {}
 
-        def score_pass(o, b, j):
-            if o == 0:
+        def score_pass(o, b, j, first):
+            if first:
                 scores[b, j] = score_ps.tile([P, N], F32, name="score", tag="acc")
             cols = slice(j * P, (j + 1) * P)
             nc.tensor.matmul_mx(
                 out=scores[b, j][:],
-                lhsT=qw[:, b, o, cols].bitcast(FP8X4),
+                lhsT=qw[b][:, o, cols].bitcast(FP8X4),
                 lhsT_scale=qs[:, b * PASSES + o, cols],
                 rhs=kw[o, b].bitcast(FP8X4),
                 rhs_scale=ks[4 * o : P, b * N : (b + 1) * N],
-                start=(o == 0),
-                stop=(o == PASSES - 1),
+                start=first,
+                stop=not first,
             )
 
         capped, neg_c, neg_m, prob = {}, {}, {}, {}
@@ -125,7 +127,9 @@ def tile_attend_soft_cap_gate_pgb2q256n512t2048_kernel(
         inv = keep.tile([P, B * QBLOCKS], F32, name="inv")
 
         def cap(i):
-            capped[i] = keep.tile([P, PACK, P], F32, name="capped%d" % i)
+            capped[i] = late.tile(
+                [P, PACK, P], F32, name="capped%d" % i, offset=36864 + 2048 * i, align_bytes=64
+            )
             nc.scalar.activation(
                 capped[i][:],
                 scores[blocks[i]][:].rearrange("q (p t) -> q t p", t=PACK),
@@ -159,7 +163,9 @@ def tile_attend_soft_cap_gate_pgb2q256n512t2048_kernel(
             bank = turn_ps.tile([P, PACK, P], F32, name="p_turned", tag="turn")
             for t in range(PACK):
                 nc.tensor.transpose(bank[:, t, :], prob[i][:, t * P : (t + 1) * P], ident[:])
-            w_bf[i] = keep.tile([P, P, PACK], BF16, name="w_bf%d" % i, align_bytes=64)
+            w_bf[i] = late.tile(
+                [P, P, PACK], BF16, name="w_bf%d" % i, offset=36864 + 2048 * ((i + 2) % 4), align_bytes=64
+            )
             nc.vector.tensor_tensor(
                 w_bf[i][:],
                 bank[:].rearrange("p t q -> p q t"),
@@ -190,7 +196,7 @@ def tile_attend_soft_cap_gate_pgb2q256n512t2048_kernel(
                 picked[:].rearrange("e u p h -> e p u h"), v_half[:].indirect(list_of(b)), ACT.Copy
             )
             words = picked[:].rearrange("e u p h -> e (u p h)").bitcast(F32)
-            bank = turn_ps.tile([P, 2, DV], F32, name="v_turned", tag="turn")
+            bank = score_ps.tile([P, 2, DV], F32, name="v_turned", tag="acc")
             for u in range(2):
                 nc.tensor.transpose(bank[:, u, :], words[:, u * P : (u + 1) * P], ident[:])
             nc.scalar.copy(
@@ -225,13 +231,20 @@ def tile_attend_soft_cap_gate_pgb2q256n512t2048_kernel(
                 stop=True,
             )
             res = keep.tile([P, DV], F32, name="res%d" % i)
-            nc.vector.scalar_tensor_tensor(res[:], y[:], inv[:, i : i + 1], gate[:, i, :], ALU.mult, ALU.mult)
+            if b == 0:
+                mean = keep.tile([P, DV], F32, name="mean%d" % i)
+                nc.scalar.activation(mean[:], y[:], ACT.Copy, scale=inv[:, i : i + 1])
+                nc.gpsimd.tensor_tensor(res[:], mean[:], gate[:, i, :], ALU.mult)
+            else:
+                nc.vector.scalar_tensor_tensor(
+                    res[:], y[:], inv[:, i : i + 1], gate[:, i, :], ALU.mult, ALU.mult
+                )
             nc.sync.dma_start(out[b, j * P : (j + 1) * P, :], res[:])
 
         vs_col = []
 
         def turn_token_scales(b):
-            bank = turn_ps.tile([P, PACK, P], F32, name="vs_turned", tag="turn")
+            bank = score_ps.tile([P, PACK, P], F32, name="vs_turned", tag="acc")
             for t in range(PACK):
                 nc.tensor.transpose(bank[:, t, :], vs_row[:, b * N + t : (b + 1) * N : PACK], ident[:])
             col = keep.tile([P, PACK], F32, name="vs_col%d" % b)
@@ -242,18 +255,20 @@ def tile_attend_soft_cap_gate_pgb2q256n512t2048_kernel(
         nc.vector.tensor_copy(vs_row[:], vs_pool[:].indirect(offsets[:]))
         nc.sync.dma_start(gate_in[:], og.rearrange("b (j q) e -> q (b j) e", q=P))
         gather_first_keys()
-        v_half = keep.tile([P, T], BF16, name="v_half")
         nc.scalar.activation(v_half[:], v_pool[:], ACT.Copy)
-        turn_values(0)
-        turn_values(1)
         turn_token_scales(0)
         turn_token_scales(1)
+        turn_values(0)
+        turn_values(1)
+        score_pass(0, 0, 0, True)
         for b in range(B):
-            for j in range(QBLOCKS):
-                score_pass(0, b, j)
             gather_second_keys(b)
             for j in range(QBLOCKS):
-                score_pass(1, b, j)
+                if (b, j) == (0, 0):
+                    score_pass(1, b, j, False)
+                else:
+                    score_pass(1, b, j, True)
+                    score_pass(0, b, j, False)
         cap(0)
         row_max(0)
         cap(1)

@@ -40,48 +40,42 @@ def tile_attend_soft_cap_gate_pgb2q256n512t2048_kernel(
         def list_of(b):
             return offsets[:, b * LIST_COLS : (b + 1) * LIST_COLS]
 
+        V_AT, KW_AT, KS_AT, HALF_AT, VS_AT = 1024, 10240, 30720, 36864, 40960
         qs = keep.tile([P, B * PASSES, NQ], U8, name="qs", align_bytes=64)
-        ident = keep.tile([P, P], F32, name="ident")
-        vs_pool = late.tile([P, T], F32, name="vs_pool", offset=0, align_bytes=64)
-        gate_in = late.tile([P, B * QBLOCKS, DV], F32, name="gate_in", offset=0, align_bytes=64)
-        v_pool = late.tile([P, T], F32, name="v_pool", offset=8192, align_bytes=64)
-        zero_words = late.tile([P, B * PASSES * NQ // 4], I32, name="zero_words", offset=16384 - 512, align_bytes=64)
-        kw_pool = late.tile([P, PASSES, T], U32, name="kw_pool", offset=16384, align_bytes=64)
-        ks_pool = late.tile([P, T], U8, name="ks_pool", offset=32768, align_bytes=64)
-        v_half = keep.tile([P, T], BF16, name="v_half")
-        qw = [
-            keep.tile([P, PASSES, NQ], U32, name="qw0", align_bytes=64),
-            late.tile([P, PASSES, NQ], U32, name="qw1", offset=32768, align_bytes=64),
-        ]
+        zero_a = late.tile([P, PASSES * NQ // 4], I32, name="zero_a", offset=V_AT - 256, align_bytes=64)
+        ident = late.tile([P, P], F32, name="ident", offset=V_AT - 512 - 64, align_bytes=64)
+        v_pool = late.tile([P, T], F32, name="v_pool", offset=V_AT, align_bytes=64)
+        zero_b = late.tile([P, PASSES * NQ // 4], I32, name="zero_b", offset=KW_AT - 256, align_bytes=64)
+        kw_pool = late.tile([P, PASSES, T], U32, name="kw_pool", offset=KW_AT, align_bytes=64)
+        ks_pool = late.tile([P, T], U8, name="ks_pool", offset=KS_AT, align_bytes=64)
+        qw = late.tile([P, B, PASSES, NQ], U32, name="qw", offset=KS_AT - 4096 + 64, align_bytes=64)
+        gate_in = late.tile([P, B * QBLOCKS, DV], F32, name="gate_in", offset=KS_AT + 1024, align_bytes=64)
+        v_half = late.tile([P, T], BF16, name="v_half", offset=HALF_AT, align_bytes=64)
+        vs_pool = late.tile([P, T], F32, name="vs_pool", offset=VS_AT, align_bytes=64)
 
-        nc.gpsimd.memset(ks_pool[:].bitcast(I32), 0)
-        nc.gpsimd.memset(vs_pool[:, :760], 0.0)
-        nc.gpsimd.memset(zero_words[:], 0)
-        nc.vector.memset(vs_pool[:, 760:1403], 0.0)
-        nc.vector.memset(vs_pool[:, 1403:], 0.0)
-        nc.vector.tensor_copy(qs[:].rearrange("p a n -> p (a n)").bitcast(I32), zero_words[:])
+        qs_words = qs[:].rearrange("p a n -> p (a n)").bitcast(I32)
+        half = PASSES * NQ // 4
+        nc.vector.memset(zero_a[:], 0)
+        nc.vector.memset(ks_pool[:].bitcast(I32), 0)
+        nc.vector.tensor_copy(qs_words[:, :half], zero_a[:])
+        nc.vector.memset(zero_b[:], 0)
+        nc.vector.memset(vs_pool[:], 0.0)
+        nc.vector.tensor_copy(qs_words[:, half:], zero_b[:])
         make_identity(nc, ident[:])
-
-        def load_keys(o):
-            nc.sync.dma_start(
-                kw_pool[:, o, :].bitcast(I32), k_words[o].rearrange("g t r -> g (t r)").bitcast(I32)
-            )
-
-        def load_queries(b):
-            nc.sync.dma_start(
-                qw[b][:].bitcast(I32), q_words[b].rearrange("o g q r -> g o (q r)").bitcast(I32)
-            )
 
         for quad in range(4):
             nc.sync.dma_start(
                 ks_pool[32 * quad : 32 * quad + 4 * PASSES, :].bitcast(I32),
                 k_scales[:, 4 * quad : 4 * quad + 4, :].bitcast(I32),
             )
-        load_queries(0)
+        for h in range(2):
+            cols = slice(h * T // 2, (h + 1) * T // 2)
+            nc.sync.dma_start(v_pool[:, cols], vT[:, cols])
         nc.sync.dma_start(vs_pool[0:1, :], vs[0:1, :])
-        nc.sync.dma_start(v_pool[:], vT)
-        load_keys(0)
-        load_keys(1)
+        for o in range(PASSES):
+            nc.sync.dma_start(
+                kw_pool[:, o, :].bitcast(I32), k_words[o].rearrange("g t r -> g (t r)").bitcast(I32)
+            )
         q_scale_rows = q_scales.rearrange("b o f n -> f (b o) n")
         for quad in range(4):
             nc.sync.dma_start(
@@ -91,12 +85,16 @@ def tile_attend_soft_cap_gate_pgb2q256n512t2048_kernel(
 
         ks = keep.tile([P, B * N], U8, name="ks", align_bytes=64)
         nc.vector.tensor_copy(ks[:], ks_pool[:].indirect(offsets[:]))
-        load_queries(1)
+        for b in range(B):
+            nc.sync.dma_start(
+                qw[:, b].bitcast(I32), q_words[b].rearrange("o g q r -> g o (q r)").bitcast(I32)
+            )
+        nc.sync.dma_start(gate_in[:], og.rearrange("b (j q) e -> q (b j) e", q=P))
 
         kw = {}
 
         def gather_first_keys():
-            both = late.tile([P, B * N], U32, name="kw0", offset=2048, align_bytes=64)
+            both = keep.tile([P, B * N], U32, name="kw0", align_bytes=64)
             nc.vector.tensor_copy(both[:], kw_pool[:, 0, :].indirect(offsets[:]))
             for b in range(B):
                 kw[0, b] = both[:, b * N : (b + 1) * N]
@@ -114,7 +112,7 @@ def tile_attend_soft_cap_gate_pgb2q256n512t2048_kernel(
             cols = slice(j * P, (j + 1) * P)
             nc.tensor.matmul_mx(
                 out=scores[b, j][:],
-                lhsT=qw[b][:, o, cols].bitcast(FP8X4),
+                lhsT=qw[:, b, o, cols].bitcast(FP8X4),
                 lhsT_scale=qs[:, b * PASSES + o, cols],
                 rhs=kw[o, b].bitcast(FP8X4),
                 rhs_scale=ks[4 * o : P, b * N : (b + 1) * N],
@@ -127,9 +125,7 @@ def tile_attend_soft_cap_gate_pgb2q256n512t2048_kernel(
         inv = keep.tile([P, B * QBLOCKS], F32, name="inv")
 
         def cap(i):
-            capped[i] = late.tile(
-                [P, PACK, P], F32, name="capped%d" % i, offset=36864 + 2048 * i, align_bytes=64
-            )
+            capped[i] = keep.tile([P, PACK, P], F32, name="capped%d" % i, align_bytes=64)
             nc.scalar.activation(
                 capped[i][:],
                 scores[blocks[i]][:].rearrange("q (p t) -> q t p", t=PACK),
@@ -163,9 +159,7 @@ def tile_attend_soft_cap_gate_pgb2q256n512t2048_kernel(
             bank = turn_ps.tile([P, PACK, P], F32, name="p_turned", tag="turn")
             for t in range(PACK):
                 nc.tensor.transpose(bank[:, t, :], prob[i][:, t * P : (t + 1) * P], ident[:])
-            w_bf[i] = late.tile(
-                [P, P, PACK], BF16, name="w_bf%d" % i, offset=36864 + 2048 * ((i + 2) % 4), align_bytes=64
-            )
+            w_bf[i] = keep.tile([P, P, PACK], BF16, name="w_bf%d" % i, align_bytes=64)
             nc.vector.tensor_tensor(
                 w_bf[i][:],
                 bank[:].rearrange("p t q -> p q t"),
@@ -187,7 +181,7 @@ def tile_attend_soft_cap_gate_pgb2q256n512t2048_kernel(
             )
 
         v_bf = keep.tile([P, B, DV, PACK], BF16, name="v_bf", align_bytes=64)
-        v_codes = keep.tile([P, B, DV], U32, name="v_codes", align_bytes=64)
+        v_codes = late.tile([P, B, DV], U32, name="v_codes", offset=KW_AT, align_bytes=64)
         v_scales = keep.tile([P, B, DV], U8, name="v_scales", align_bytes=64)
 
         def turn_values(b):
@@ -196,7 +190,7 @@ def tile_attend_soft_cap_gate_pgb2q256n512t2048_kernel(
                 picked[:].rearrange("e u p h -> e p u h"), v_half[:].indirect(list_of(b)), ACT.Copy
             )
             words = picked[:].rearrange("e u p h -> e (u p h)").bitcast(F32)
-            bank = score_ps.tile([P, 2, DV], F32, name="v_turned", tag="acc")
+            bank = turn_ps.tile([P, 2, DV], F32, name="v_turned", tag="turn")
             for u in range(2):
                 nc.tensor.transpose(bank[:, u, :], words[:, u * P : (u + 1) * P], ident[:])
             nc.scalar.copy(
@@ -244,48 +238,47 @@ def tile_attend_soft_cap_gate_pgb2q256n512t2048_kernel(
         vs_col = []
 
         def turn_token_scales(b):
-            bank = score_ps.tile([P, PACK, P], F32, name="vs_turned", tag="acc")
+            bank = turn_ps.tile([P, PACK, P], F32, name="vs_turned", tag="turn")
             for t in range(PACK):
-                nc.tensor.transpose(bank[:, t, :], vs_row[:, b * N + t : (b + 1) * N : PACK], ident[:])
-            col = keep.tile([P, PACK], F32, name="vs_col%d" % b)
+                nc.tensor.transpose(bank[:, t, :], vs_row[b][:, t:N:PACK], ident[:])
+            col = late.tile([P, PACK], F32, name="vs_col%d" % b, offset=HALF_AT + 64 * b, align_bytes=64)
             nc.scalar.activation(col[:], bank[:, :, 0], ACT.Copy)
             vs_col.append(col)
 
-        vs_row = keep.tile([P, B * N], F32, name="vs_row")
-        nc.vector.tensor_copy(vs_row[:], vs_pool[:].indirect(offsets[:]))
-        nc.sync.dma_start(gate_in[:], og.rearrange("b (j q) e -> q (b j) e", q=P))
+        vs_row = []
+        for b in range(B):
+            vs_row.append(keep.tile([P, N], F32, name="vs_row%d" % b))
+            nc.vector.tensor_copy(vs_row[b][:], vs_pool[:].indirect(list_of(b)))
         gather_first_keys()
-        nc.scalar.activation(v_half[:], v_pool[:], ACT.Copy)
-        turn_token_scales(0)
-        turn_token_scales(1)
+        for h in range(2):
+            cols = slice(h * T // 2, (h + 1) * T // 2)
+            nc.scalar.activation(v_half[:, cols], v_pool[:, cols], ACT.Copy)
         turn_values(0)
         turn_values(1)
-        score_pass(0, 0, 0, True)
+        turn_token_scales(0)
+        turn_token_scales(1)
         for b in range(B):
             gather_second_keys(b)
             for j in range(QBLOCKS):
-                if (b, j) == (0, 0):
-                    score_pass(1, b, j, False)
-                else:
-                    score_pass(1, b, j, True)
-                    score_pass(0, b, j, False)
+                score_pass(0, b, j, True)
+                score_pass(1, b, j, False)
+        make_gate()
+        quantise_v()
         cap(0)
         row_max(0)
         cap(1)
-        make_gate()
-        exponent(0)
         row_max(1)
         cap(2)
-        exponent(1)
         row_max(2)
+        exponent(0)
         cap(3)
-        exponent(2)
         row_max(3)
+        exponent(1)
         weigh(0)
-        exponent(3)
-        quantise_v()
+        exponent(2)
         weigh(1)
         quantise_w(0)
+        exponent(3)
         invert(0)
         weigh(2)
         quantise_w(1)

@@ -40,7 +40,7 @@ def tile_attend_soft_cap_gate_pgb2q256n512t2048_kernel(
         def list_of(b):
             return offsets[:, b * LIST_COLS : (b + 1) * LIST_COLS]
 
-        V_AT, KW_AT, KS_AT, HALF_AT, VS_AT = 1024, 10240, 30720, 36864, 40960
+        V_AT, KW_AT, KS_AT, HALF_AT, VS_AT, LAST_AT = 1024, 10240, 30720, 36864, 40960, 49152
         qs = keep.tile([P, B * PASSES, NQ], U8, name="qs", align_bytes=64)
         zero_a = late.tile([P, PASSES * NQ // 4], I32, name="zero_a", offset=V_AT - 256, align_bytes=64)
         ident = late.tile([P, P], F32, name="ident", offset=V_AT - 512 - 64, align_bytes=64)
@@ -134,7 +134,7 @@ def tile_attend_soft_cap_gate_pgb2q256n512t2048_kernel(
             )
 
         def row_max(i):
-            neg_c[i] = keep.tile([P, N], F32, name="neg_c%d" % i)
+            neg_c[i] = late.tile([P, N], F32, name="neg_c%d" % i, offset=LAST_AT + 2048 * (3 - i), align_bytes=64)
             neg_m[i] = keep.tile([P, 1], F32, name="neg_m%d" % i)
             nc.vector.tensor_scalar(
                 neg_c[i][:],
@@ -205,12 +205,12 @@ def tile_attend_soft_cap_gate_pgb2q256n512t2048_kernel(
                 in_=v_bf[:].rearrange("p b e t -> p (b e t)"),
             )
 
-        gate_tanh = keep.tile([P, B * QBLOCKS, DV], F32, name="gate_tanh")
+        gate_tanh = late.tile([P, B * QBLOCKS, DV], F32, name="gate_tanh", offset=LAST_AT, align_bytes=64)
         gate = keep.tile([P, B * QBLOCKS, DV], F32, name="gate")
 
         def make_gate():
             nc.scalar.activation(gate_tanh[:], gate_in[:], ACT.Tanh, scale=0.5)
-            nc.gpsimd.tensor_scalar(gate[:], gate_tanh[:], 0.5, 0.5, ALU.mult, ALU.add)
+            nc.scalar.activation(gate[:], gate_tanh[:], ACT.Copy, bias=0.5, scale=0.5)
 
         def finish(i):
             b, j = blocks[i]
@@ -225,14 +225,7 @@ def tile_attend_soft_cap_gate_pgb2q256n512t2048_kernel(
                 stop=True,
             )
             res = keep.tile([P, DV], F32, name="res%d" % i)
-            if b == 0:
-                mean = keep.tile([P, DV], F32, name="mean%d" % i)
-                nc.scalar.activation(mean[:], y[:], ACT.Copy, scale=inv[:, i : i + 1])
-                nc.gpsimd.tensor_tensor(res[:], mean[:], gate[:, i, :], ALU.mult)
-            else:
-                nc.vector.scalar_tensor_tensor(
-                    res[:], y[:], inv[:, i : i + 1], gate[:, i, :], ALU.mult, ALU.mult
-                )
+            nc.vector.scalar_tensor_tensor(res[:], y[:], inv[:, i : i + 1], gate[:, i, :], ALU.mult, ALU.mult)
             nc.sync.dma_start(out[b, j * P : (j + 1) * P, :], res[:])
 
         vs_col = []
@@ -262,7 +255,6 @@ def tile_attend_soft_cap_gate_pgb2q256n512t2048_kernel(
             for j in range(QBLOCKS):
                 score_pass(0, b, j, True)
                 score_pass(1, b, j, False)
-        make_gate()
         quantise_v()
         cap(0)
         row_max(0)
@@ -279,14 +271,15 @@ def tile_attend_soft_cap_gate_pgb2q256n512t2048_kernel(
         weigh(1)
         quantise_w(0)
         exponent(3)
+        make_gate()
         invert(0)
         weigh(2)
         quantise_w(1)
-        finish(0)
         weigh(3)
         quantise_w(2)
-        finish(1)
         invert(1)
+        finish(0)
         quantise_w(3)
+        finish(1)
         finish(2)
         finish(3)

@@ -49,7 +49,7 @@ def tile_attend_soft_cap_gate_pgb2q256n512t2048_kernel(
         kw_pool = late.tile([P, PASSES, T], U32, name="kw_pool", offset=KW_AT, align_bytes=64)
         ks_pool = late.tile([P, T], U8, name="ks_pool", offset=KS_AT, align_bytes=64)
         qw = late.tile([P, B, PASSES, NQ], U32, name="qw", offset=KS_AT - 4096 + 64, align_bytes=64)
-        gate_in = late.tile([P, B * QBLOCKS, DV], F32, name="gate_in", offset=KS_AT + 1024, align_bytes=64)
+        gate_in = late.tile([P, B * QBLOCKS, DV], F32, name="gate_in", offset=VS_AT, align_bytes=64)
         v_half = late.tile([P, T], BF16, name="v_half", offset=HALF_AT, align_bytes=64)
         vs_pool = late.tile([P, T], F32, name="vs_pool", offset=VS_AT, align_bytes=64)
 
@@ -63,11 +63,17 @@ def tile_attend_soft_cap_gate_pgb2q256n512t2048_kernel(
         nc.vector.tensor_copy(qs_words[:, half:], zero_b[:])
         make_identity(nc, ident[:])
 
-        for quad in range(4):
+        for quad in range(2):
             nc.sync.dma_start(
                 ks_pool[32 * quad : 32 * quad + 4 * PASSES, :].bitcast(I32),
                 k_scales[:, 4 * quad : 4 * quad + 4, :].bitcast(I32),
             )
+        for quad in range(2, 4):
+            for o in range(PASSES):
+                nc.sync.dma_start(
+                    ks_pool[32 * quad + 4 * o : 32 * quad + 4 * o + 4, :].bitcast(I32),
+                    k_scales[o, 4 * quad : 4 * quad + 4, :].bitcast(I32),
+                )
         for h in range(2):
             cols = slice(h * T // 2, (h + 1) * T // 2)
             nc.sync.dma_start(v_pool[:, cols], vT[:, cols])
@@ -89,19 +95,25 @@ def tile_attend_soft_cap_gate_pgb2q256n512t2048_kernel(
             nc.sync.dma_start(
                 qw[:, b].bitcast(I32), q_words[b].rearrange("o g q r -> g o (q r)").bitcast(I32)
             )
-        nc.sync.dma_start(gate_in[:], og.rearrange("b (j q) e -> q (b j) e", q=P))
 
         kw = {}
 
-        def gather_first_keys():
-            both = keep.tile([P, B * N], U32, name="kw0", align_bytes=64)
-            nc.vector.tensor_copy(both[:], kw_pool[:, 0, :].indirect(offsets[:]))
-            for b in range(B):
-                kw[0, b] = both[:, b * N : (b + 1) * N]
+        def gather_keys(o, b):
+            kw[o, b] = keep.tile([P, N], U32, name="kw%d%d" % (o, b), align_bytes=64)[:]
+            nc.vector.tensor_copy(kw[o, b], kw_pool[:, o, :].indirect(list_of(b)))
 
-        def gather_second_keys(b):
-            kw[1, b] = keep.tile([P, N], U32, name="kw1%d" % b, align_bytes=64)[:]
-            nc.vector.tensor_copy(kw[1, b], kw_pool[:, 1, :].indirect(list_of(b)))
+        def warm_up():
+            idle = turn_ps.tile([P, N], F32, name="idle", tag="turn")
+            for first in (True, False):
+                nc.tensor.matmul_mx(
+                    out=idle[:],
+                    lhsT=kw[0, 0][:, :P].bitcast(FP8X4),
+                    lhsT_scale=ks[:, :P],
+                    rhs=kw[0, 0].bitcast(FP8X4),
+                    rhs_scale=ks[:, :N],
+                    start=first,
+                    stop=not first,
+                )
 
         blocks = [(b, j) for b in range(B) for j in range(QBLOCKS)]
         scores = {}
@@ -185,14 +197,12 @@ def tile_attend_soft_cap_gate_pgb2q256n512t2048_kernel(
         v_scales = keep.tile([P, B, DV], U8, name="v_scales", align_bytes=64)
 
         def turn_values(b):
-            picked = keep.tile([P, 2, P, 2], BF16, name="v_picked%d" % b)
-            nc.scalar.activation(
-                picked[:].rearrange("e u p h -> e p u h"), v_half[:].indirect(list_of(b)), ACT.Copy
-            )
-            words = picked[:].rearrange("e u p h -> e (u p h)").bitcast(F32)
+            picked = keep.tile([P, N], BF16, name="v_picked%d" % b)
+            nc.scalar.activation(picked[:], v_half[:].indirect(list_of(b)), ACT.Copy)
+            words = picked[:].bitcast(F32)
             bank = turn_ps.tile([P, 2, DV], F32, name="v_turned", tag="turn")
             for u in range(2):
-                nc.tensor.transpose(bank[:, u, :], words[:, u * P : (u + 1) * P], ident[:])
+                nc.tensor.transpose(bank[:, u, :], words[:, u : 2 * P : 2], ident[:])
             nc.scalar.copy(
                 v_bf[:, b].rearrange("p e t -> p (e t)").bitcast(F32).rearrange("p (e u) -> p e u", u=2),
                 bank[:].rearrange("p u e -> p e u"),
@@ -228,30 +238,25 @@ def tile_attend_soft_cap_gate_pgb2q256n512t2048_kernel(
             nc.vector.scalar_tensor_tensor(res[:], y[:], inv[:, i : i + 1], gate[:, i, :], ALU.mult, ALU.mult)
             nc.sync.dma_start(out[b, j * P : (j + 1) * P, :], res[:])
 
-        vs_col = []
-
-        def turn_token_scales(b):
-            bank = turn_ps.tile([P, PACK, P], F32, name="vs_turned", tag="turn")
-            for t in range(PACK):
-                nc.tensor.transpose(bank[:, t, :], vs_row[b][:, t:N:PACK], ident[:])
-            col = late.tile([P, PACK], F32, name="vs_col%d" % b, offset=HALF_AT + 64 * b, align_bytes=64)
-            nc.scalar.activation(col[:], bank[:, :, 0], ACT.Copy)
-            vs_col.append(col)
-
-        vs_row = []
-        for b in range(B):
-            vs_row.append(keep.tile([P, N], F32, name="vs_row%d" % b))
-            nc.vector.tensor_copy(vs_row[b][:], vs_pool[:].indirect(list_of(b)))
-        gather_first_keys()
+        vs_row = keep.tile([P, B * N], F32, name="vs_row")
+        nc.vector.tensor_copy(vs_row[:], vs_pool[:].indirect(offsets[:]))
+        nc.sync.dma_start(gate_in[:], og.rearrange("b (j q) e -> q (b j) e", q=P))
+        gather_keys(0, 0)
+        warm_up()
+        gather_keys(0, 1)
         for h in range(2):
             cols = slice(h * T // 2, (h + 1) * T // 2)
             nc.scalar.activation(v_half[:, cols], v_pool[:, cols], ACT.Copy)
         turn_values(0)
         turn_values(1)
-        turn_token_scales(0)
-        turn_token_scales(1)
+        vs_col = []
         for b in range(B):
-            gather_second_keys(b)
+            vs_col.append(late.tile([P, PACK], F32, name="vs_col%d" % b, offset=HALF_AT + 64 * b, align_bytes=64))
+            nc.sync.dma_start(
+                vs_col[b][:], vs_row[0:1, b * N : (b + 1) * N].rearrange("o (p t) -> o p t", t=PACK)
+            )
+        for b in range(B):
+            gather_keys(1, b)
             for j in range(QBLOCKS):
                 score_pass(0, b, j, True)
                 score_pass(1, b, j, False)

@@ -32,7 +32,8 @@ def tile_attend_soft_cap_gate_pgb2q256n512t2048_kernel(
         keep = ctx.enter_context(tc.tile_pool(name="keep", bufs=1))
         late = ctx.enter_context(tc.tile_pool(name="late", bufs=1))
         score_ps = ctx.enter_context(tc.psum_pool(name="score_ps", bufs=4))
-        turn_ps = ctx.enter_context(tc.psum_pool(name="turn_ps", bufs=4))
+        turn_ps = ctx.enter_context(tc.psum_pool(name="turn_ps", bufs=3))
+        early_ps = ctx.enter_context(tc.psum_pool(name="early_ps", bufs=1))
 
         offsets = keep.tile([P, B * LIST_COLS], U16, name="offsets")
         nc.sync.dma_start(offsets[:], offs)
@@ -40,67 +41,80 @@ def tile_attend_soft_cap_gate_pgb2q256n512t2048_kernel(
         def list_of(b):
             return offsets[:, b * LIST_COLS : (b + 1) * LIST_COLS]
 
-        V_AT, KW_AT, KS_AT, HALF_AT, VS_AT, LAST_AT = 1024, 10240, 30720, 36864, 40960, 49152
+        ZERO_AT, KW_AT, KS_AT, HALF_AT, VS_AT, LAST_AT = 1024, 1920, 14336, 26624, 32768, 49152
+        KW1_AT = KS_AT + T - 64
+        DENSE = P - PASSES * 16
+        v_pool = keep.tile([P, T], F32, name="v_pool")
+        ks = keep.tile([P, B * N], U8, name="ks", align_bytes=64)
+        zeros = late.tile([P, B * N // 4 + 1], I32, name="zeros", offset=ZERO_AT, align_bytes=64)
+        ident = late.tile([P, P], F32, name="ident", offset=ZERO_AT - 448, align_bytes=64)
+        kw_pool = [
+            late.tile([P, T], U32, name="kw_pool0", offset=KW_AT, align_bytes=64),
+            late.tile([P, T], U32, name="kw_pool1", offset=KW1_AT, align_bytes=64),
+        ]
+        ks_pool = late.tile([P, T + 4], U8, name="ks_pool", offset=KS_AT, align_bytes=64)
         qs = keep.tile([P, B * PASSES, NQ], U8, name="qs", align_bytes=64)
-        zero_a = late.tile([P, PASSES * NQ // 4], I32, name="zero_a", offset=V_AT - 256, align_bytes=64)
-        ident = late.tile([P, P], F32, name="ident", offset=V_AT - 512 - 64, align_bytes=64)
-        v_pool = late.tile([P, T], F32, name="v_pool", offset=V_AT, align_bytes=64)
-        zero_b = late.tile([P, PASSES * NQ // 4], I32, name="zero_b", offset=KW_AT - 256, align_bytes=64)
-        kw_pool = late.tile([P, PASSES, T], U32, name="kw_pool", offset=KW_AT, align_bytes=64)
-        ks_pool = late.tile([P, T], U8, name="ks_pool", offset=KS_AT, align_bytes=64)
         qw = late.tile([P, B, PASSES, NQ], U32, name="qw", offset=KS_AT - 4096 + 64, align_bytes=64)
-        gate_in = late.tile([P, B * QBLOCKS, DV], F32, name="gate_in", offset=VS_AT, align_bytes=64)
+        gate_in = late.tile([P, B * QBLOCKS, DV], F32, name="gate_in", offset=KW_AT + 4096, align_bytes=64)
         v_half = late.tile([P, T], BF16, name="v_half", offset=HALF_AT, align_bytes=64)
-        vs_pool = late.tile([P, T], F32, name="vs_pool", offset=VS_AT, align_bytes=64)
+        vs_pool = late.tile([P, T + 1], F32, name="vs_pool", offset=VS_AT, align_bytes=64)
 
-        qs_words = qs[:].rearrange("p a n -> p (a n)").bitcast(I32)
-        half = PASSES * NQ // 4
-        nc.vector.memset(zero_a[:], 0)
-        nc.vector.memset(ks_pool[:].bitcast(I32), 0)
-        nc.vector.tensor_copy(qs_words[:, :half], zero_a[:])
-        nc.vector.memset(zero_b[:], 0)
-        nc.vector.memset(vs_pool[:], 0.0)
-        nc.vector.tensor_copy(qs_words[:, half:], zero_b[:])
-        make_identity(nc, ident[:])
-
-        for quad in range(2):
-            nc.sync.dma_start(
-                ks_pool[32 * quad : 32 * quad + 4 * PASSES, :].bitcast(I32),
-                k_scales[:, 4 * quad : 4 * quad + 4, :].bitcast(I32),
-            )
-        for quad in range(2, 4):
-            for o in range(PASSES):
-                nc.sync.dma_start(
-                    ks_pool[32 * quad + 4 * o : 32 * quad + 4 * o + 4, :].bitcast(I32),
-                    k_scales[o, 4 * quad : 4 * quad + 4, :].bitcast(I32),
-                )
+        nc.sync.dma_start(
+            ks_pool[DENSE:P, :T].bitcast(I32), k_scales.rearrange("o f t -> (o f) t").bitcast(I32)
+        )
         for h in range(2):
             cols = slice(h * T // 2, (h + 1) * T // 2)
             nc.sync.dma_start(v_pool[:, cols], vT[:, cols])
-        nc.sync.dma_start(vs_pool[0:1, :], vs[0:1, :])
-        for o in range(PASSES):
+
+        nc.vector.memset(zeros[:], 0)
+        nc.vector.memset(ks_pool[0:DENSE, :].bitcast(I32), 0)
+        nc.gpsimd.memset(vs_pool[:, :1408].bitcast(I32), 0)
+        nc.vector.memset(vs_pool[:, 1408:].bitcast(I32), 0)
+        nc.vector.tensor_copy(ks[:].bitcast(I32), zeros[:, : B * N // 4])
+        nc.vector.tensor_copy(qs[:].rearrange("p a n -> p (a n)").bitcast(I32), zeros[:, : B * N // 4])
+        make_identity(nc, ident[:])
+
+        def load_keys(o):
             nc.sync.dma_start(
-                kw_pool[:, o, :].bitcast(I32), k_words[o].rearrange("g t r -> g (t r)").bitcast(I32)
+                kw_pool[o][:].bitcast(I32), k_words[o].rearrange("g t r -> g (t r)").bitcast(I32)
             )
+
+        def load_queries(b):
+            nc.sync.dma_start(
+                qw[:, b].bitcast(I32), q_words[b].rearrange("o g q r -> g o (q r)").bitcast(I32)
+            )
+
+        nc.sync.dma_start(vs_pool[0:1, :T], vs[0:1, :])
         q_scale_rows = q_scales.rearrange("b o f n -> f (b o) n")
         for quad in range(4):
             nc.sync.dma_start(
                 qs[32 * quad : 32 * quad + 4, :, :].bitcast(I32),
                 q_scale_rows[4 * quad : 4 * quad + 4].bitcast(I32),
             )
+        load_keys(0)
 
-        ks = keep.tile([P, B * N], U8, name="ks", align_bytes=64)
-        nc.vector.tensor_copy(ks[:], ks_pool[:].indirect(offsets[:]))
-        for b in range(B):
-            nc.sync.dma_start(
-                qw[:, b].bitcast(I32), q_words[b].rearrange("o g q r -> g o (q r)").bitcast(I32)
-            )
+        ks_dense = keep.tile([P, B * N], U8, name="ks_dense", align_bytes=64)
+        nc.vector.tensor_copy(ks_dense[:], ks_pool[:, :T].indirect(offsets[:]))
+
+        def place_key_scales(o, quad):
+            src = DENSE + 16 * o + 4 * quad
+            dst = 32 * quad + 4 * o
+            nc.sync.dma_start(ks[dst : dst + 4, :].bitcast(I32), ks_dense[src : src + 4, :].bitcast(I32))
+
+        places = [(o, quad) for o in range(PASSES) for quad in range(4)]
+        for o, quad in places[:3]:
+            place_key_scales(o, quad)
+        load_keys(1)
+        for o, quad in places[3:]:
+            place_key_scales(o, quad)
+        load_queries(0)
+        load_queries(1)
 
         kw = {}
 
         def gather_keys(o, b):
             kw[o, b] = keep.tile([P, N], U32, name="kw%d%d" % (o, b), align_bytes=64)[:]
-            nc.vector.tensor_copy(kw[o, b], kw_pool[:, o, :].indirect(list_of(b)))
+            nc.vector.tensor_copy(kw[o, b], kw_pool[o][:].indirect(list_of(b)))
 
         def warm_up():
             idle = turn_ps.tile([P, N], F32, name="idle", tag="turn")
@@ -108,9 +122,9 @@ def tile_attend_soft_cap_gate_pgb2q256n512t2048_kernel(
                 nc.tensor.matmul_mx(
                     out=idle[:],
                     lhsT=kw[0, 0][:, :P].bitcast(FP8X4),
-                    lhsT_scale=ks[:, :P],
+                    lhsT_scale=ks_dense[:, :P],
                     rhs=kw[0, 0].bitcast(FP8X4),
-                    rhs_scale=ks[:, :N],
+                    rhs_scale=ks_dense[:, :N],
                     start=first,
                     stop=not first,
                 )
@@ -193,19 +207,21 @@ def tile_attend_soft_cap_gate_pgb2q256n512t2048_kernel(
             )
 
         v_bf = keep.tile([P, B, DV, PACK], BF16, name="v_bf", align_bytes=64)
-        v_codes = late.tile([P, B, DV], U32, name="v_codes", offset=KW_AT, align_bytes=64)
+        v_codes = late.tile([P, B, DV], U32, name="v_codes", offset=KW1_AT, align_bytes=64)
         v_scales = keep.tile([P, B, DV], U8, name="v_scales", align_bytes=64)
+
+        v_turned = early_ps.tile([P, B, 2, DV], F32, name="v_turned", tag="early")
 
         def turn_values(b):
             picked = keep.tile([P, N], BF16, name="v_picked%d" % b)
             nc.scalar.activation(picked[:], v_half[:].indirect(list_of(b)), ACT.Copy)
             words = picked[:].bitcast(F32)
-            bank = turn_ps.tile([P, 2, DV], F32, name="v_turned", tag="turn")
+            bank = v_turned[:, b]
             for u in range(2):
                 nc.tensor.transpose(bank[:, u, :], words[:, u : 2 * P : 2], ident[:])
             nc.scalar.copy(
                 v_bf[:, b].rearrange("p e t -> p (e t)").bitcast(F32).rearrange("p (e u) -> p e u", u=2),
-                bank[:].rearrange("p u e -> p e u"),
+                bank.rearrange("p u e -> p e u"),
             )
 
         def quantise_v():
@@ -239,16 +255,16 @@ def tile_attend_soft_cap_gate_pgb2q256n512t2048_kernel(
             nc.sync.dma_start(out[b, j * P : (j + 1) * P, :], res[:])
 
         vs_row = keep.tile([P, B * N], F32, name="vs_row")
-        nc.vector.tensor_copy(vs_row[:], vs_pool[:].indirect(offsets[:]))
-        nc.sync.dma_start(gate_in[:], og.rearrange("b (j q) e -> q (b j) e", q=P))
+        nc.vector.tensor_copy(vs_row[:], vs_pool[:, :T].indirect(offsets[:]))
         gather_keys(0, 0)
-        warm_up()
         gather_keys(0, 1)
+        nc.sync.dma_start(gate_in[:], og.rearrange("b (j q) e -> q (b j) e", q=P))
         for h in range(2):
             cols = slice(h * T // 2, (h + 1) * T // 2)
             nc.scalar.activation(v_half[:, cols], v_pool[:, cols], ACT.Copy)
         turn_values(0)
         turn_values(1)
+        warm_up()
         vs_col = []
         for b in range(B):
             vs_col.append(late.tile([P, PACK], F32, name="vs_col%d" % b, offset=HALF_AT + 64 * b, align_bytes=64))

@@ -32,8 +32,7 @@ def tile_attend_soft_cap_gate_pgb2q256n512t2048_kernel(
         keep = ctx.enter_context(tc.tile_pool(name="keep", bufs=1))
         late = ctx.enter_context(tc.tile_pool(name="late", bufs=1))
         score_ps = ctx.enter_context(tc.psum_pool(name="score_ps", bufs=4))
-        turn_ps = ctx.enter_context(tc.psum_pool(name="turn_ps", bufs=3))
-        early_ps = ctx.enter_context(tc.psum_pool(name="early_ps", bufs=1))
+        turn_ps = ctx.enter_context(tc.psum_pool(name="turn_ps", bufs=1))
 
         offsets = keep.tile([P, B * LIST_COLS], U16, name="offsets")
         nc.sync.dma_start(offsets[:], offs)
@@ -41,37 +40,42 @@ def tile_attend_soft_cap_gate_pgb2q256n512t2048_kernel(
         def list_of(b):
             return offsets[:, b * LIST_COLS : (b + 1) * LIST_COLS]
 
-        ZERO_AT, KW_AT, KS_AT, HALF_AT, VS_AT, LAST_AT = 1024, 1920, 14336, 26624, 32768, 49152
-        KW1_AT = KS_AT + T - 64
+        KW1_AT, Q0_AT, KS_AT, HALF_AT, VS_AT, LAST_AT = 0, 8192, 12288, 26624, 32768, 49152
         DENSE = P - PASSES * 16
+        VS_ROW = P - 1
+        VS_GPSIMD = 1000
         v_pool = keep.tile([P, T], F32, name="v_pool")
-        ks = keep.tile([P, B * N], U8, name="ks", align_bytes=64)
-        zeros = late.tile([P, B * N // 4 + 1], I32, name="zeros", offset=ZERO_AT, align_bytes=64)
-        ident = late.tile([P, P], F32, name="ident", offset=ZERO_AT - 448, align_bytes=64)
+        ks = keep.tile([P, PASSES, B * N], U8, name="ks", align_bytes=64)
+        zeros = late.tile([P, NQ // 4], I32, name="zeros", offset=Q0_AT - 128, align_bytes=64)
+        ident = keep.tile([P, P], F32, name="ident")
         kw_pool = [
-            late.tile([P, T], U32, name="kw_pool0", offset=KW_AT, align_bytes=64),
+            keep.tile([P, T], U32, name="kw_pool0", align_bytes=64),
             late.tile([P, T], U32, name="kw_pool1", offset=KW1_AT, align_bytes=64),
         ]
         ks_pool = late.tile([P, T + 4], U8, name="ks_pool", offset=KS_AT, align_bytes=64)
-        qs = keep.tile([P, B * PASSES, NQ], U8, name="qs", align_bytes=64)
-        qw = late.tile([P, B, PASSES, NQ], U32, name="qw", offset=KS_AT - 4096 + 64, align_bytes=64)
-        gate_in = late.tile([P, B * QBLOCKS, DV], F32, name="gate_in", offset=KW_AT + 4096, align_bytes=64)
+        qs = keep.tile([P, NQ], U8, name="qs", align_bytes=64)
+        qw = [
+            late.tile([P, PASSES, NQ], U32, name="qw0", offset=Q0_AT, align_bytes=64),
+            late.tile([P, PASSES, NQ], U32, name="qw1", offset=KS_AT, align_bytes=64),
+        ]
+        gate_in = late.tile([P, B * QBLOCKS, DV], F32, name="gate_in", offset=VS_AT, align_bytes=64)
         v_half = late.tile([P, T], BF16, name="v_half", offset=HALF_AT, align_bytes=64)
         vs_pool = late.tile([P, T + 1], F32, name="vs_pool", offset=VS_AT, align_bytes=64)
 
         nc.sync.dma_start(
-            ks_pool[DENSE:P, :T].bitcast(I32), k_scales.rearrange("o f t -> (o f) t").bitcast(I32)
+            ks_pool[DENSE:P, :T].bitcast(I32), k_scales.rearrange("o f t -> f o t").bitcast(I32)
         )
+        nc.sync.dma_start(vs_pool[VS_ROW:P, :T], vs[0:1, :])
         for h in range(2):
             cols = slice(h * T // 2, (h + 1) * T // 2)
             nc.sync.dma_start(v_pool[:, cols], vT[:, cols])
 
-        nc.vector.memset(zeros[:], 0)
+        nc.gpsimd.memset(zeros[:], 0)
+        nc.gpsimd.tensor_copy(qs[:].bitcast(I32), zeros[:])
         nc.vector.memset(ks_pool[0:DENSE, :].bitcast(I32), 0)
-        nc.gpsimd.memset(vs_pool[:, :1408].bitcast(I32), 0)
-        nc.vector.memset(vs_pool[:, 1408:].bitcast(I32), 0)
-        nc.vector.tensor_copy(ks[:].bitcast(I32), zeros[:, : B * N // 4])
-        nc.vector.tensor_copy(qs[:].rearrange("p a n -> p (a n)").bitcast(I32), zeros[:, : B * N // 4])
+        nc.gpsimd.memset(vs_pool[0:VS_ROW, :VS_GPSIMD].bitcast(I32), 0)
+        nc.vector.memset(vs_pool[0:VS_ROW, VS_GPSIMD:].bitcast(I32), 0)
+        nc.gpsimd.memset(ks[:].rearrange("p o n -> p (o n)").bitcast(I32), 0)
         make_identity(nc, ident[:])
 
         def load_keys(o):
@@ -81,33 +85,27 @@ def tile_attend_soft_cap_gate_pgb2q256n512t2048_kernel(
 
         def load_queries(b):
             nc.sync.dma_start(
-                qw[:, b].bitcast(I32), q_words[b].rearrange("o g q r -> g o (q r)").bitcast(I32)
+                qw[b][:].bitcast(I32), q_words[b].rearrange("o g q r -> g o (q r)").bitcast(I32)
             )
 
-        nc.sync.dma_start(vs_pool[0:1, :T], vs[0:1, :])
-        q_scale_rows = q_scales.rearrange("b o f n -> f (b o) n")
+        load_keys(0)
+        q_scale_rows = q_scales.rearrange("b o f n -> (b o) f n")
         for quad in range(4):
             nc.sync.dma_start(
-                qs[32 * quad : 32 * quad + 4, :, :].bitcast(I32),
-                q_scale_rows[4 * quad : 4 * quad + 4].bitcast(I32),
+                qs[32 * quad : 32 * quad + 16, :].bitcast(I32),
+                q_scale_rows[:, 4 * quad : 4 * quad + 4, :].bitcast(I32),
             )
-        load_keys(0)
+        load_keys(1)
+        load_queries(0)
 
         ks_dense = keep.tile([P, B * N], U8, name="ks_dense", align_bytes=64)
         nc.vector.tensor_copy(ks_dense[:], ks_pool[:, :T].indirect(offsets[:]))
 
-        def place_key_scales(o, quad):
-            src = DENSE + 16 * o + 4 * quad
-            dst = 32 * quad + 4 * o
-            nc.sync.dma_start(ks[dst : dst + 4, :].bitcast(I32), ks_dense[src : src + 4, :].bitcast(I32))
-
-        places = [(o, quad) for o in range(PASSES) for quad in range(4)]
-        for o, quad in places[:3]:
-            place_key_scales(o, quad)
-        load_keys(1)
-        for o, quad in places[3:]:
-            place_key_scales(o, quad)
-        load_queries(0)
+        for quad in range(4):
+            nc.sync.dma_start(
+                ks[32 * quad : 32 * quad + 4].bitcast(I32),
+                ks_dense[DENSE + 8 * quad : DENSE + 8 * quad + 8, :].bitcast(I32),
+            )
         load_queries(1)
 
         kw = {}
@@ -117,7 +115,7 @@ def tile_attend_soft_cap_gate_pgb2q256n512t2048_kernel(
             nc.vector.tensor_copy(kw[o, b], kw_pool[o][:].indirect(list_of(b)))
 
         def warm_up():
-            idle = turn_ps.tile([P, N], F32, name="idle", tag="turn")
+            idle = turn_ps.tile([P, N], F32, name="idle", tag="turn0")
             for first in (True, False):
                 nc.tensor.matmul_mx(
                     out=idle[:],
@@ -138,10 +136,10 @@ def tile_attend_soft_cap_gate_pgb2q256n512t2048_kernel(
             cols = slice(j * P, (j + 1) * P)
             nc.tensor.matmul_mx(
                 out=scores[b, j][:],
-                lhsT=qw[:, b, o, cols].bitcast(FP8X4),
-                lhsT_scale=qs[:, b * PASSES + o, cols],
+                lhsT=qw[b][:, o, cols].bitcast(FP8X4),
+                lhsT_scale=qs[4 * (b * PASSES + o) : P, cols],
                 rhs=kw[o, b].bitcast(FP8X4),
-                rhs_scale=ks[4 * o : P, b * N : (b + 1) * N],
+                rhs_scale=ks[:, o, b * N : (b + 1) * N],
                 start=first,
                 stop=not first,
             )
@@ -182,7 +180,7 @@ def tile_attend_soft_cap_gate_pgb2q256n512t2048_kernel(
 
         def weigh(i):
             b = blocks[i][0]
-            bank = turn_ps.tile([P, PACK, P], F32, name="p_turned", tag="turn")
+            bank = turn_ps.tile([P, PACK, P], F32, name="p_turned", tag="turn%d" % ((i + 2) % 4))
             for t in range(PACK):
                 nc.tensor.transpose(bank[:, t, :], prob[i][:, t * P : (t + 1) * P], ident[:])
             w_bf[i] = keep.tile([P, P, PACK], BF16, name="w_bf%d" % i, align_bytes=64)
@@ -210,13 +208,11 @@ def tile_attend_soft_cap_gate_pgb2q256n512t2048_kernel(
         v_codes = late.tile([P, B, DV], U32, name="v_codes", offset=KW1_AT, align_bytes=64)
         v_scales = keep.tile([P, B, DV], U8, name="v_scales", align_bytes=64)
 
-        v_turned = early_ps.tile([P, B, 2, DV], F32, name="v_turned", tag="early")
-
         def turn_values(b):
             picked = keep.tile([P, N], BF16, name="v_picked%d" % b)
             nc.scalar.activation(picked[:], v_half[:].indirect(list_of(b)), ACT.Copy)
             words = picked[:].bitcast(F32)
-            bank = v_turned[:, b]
+            bank = turn_ps.tile([P, 2, DV], F32, name="v_turned", tag="turn%d" % b)[:]
             for u in range(2):
                 nc.tensor.transpose(bank[:, u, :], words[:, u : 2 * P : 2], ident[:])
             nc.scalar.copy(
@@ -258,7 +254,6 @@ def tile_attend_soft_cap_gate_pgb2q256n512t2048_kernel(
         nc.vector.tensor_copy(vs_row[:], vs_pool[:, :T].indirect(offsets[:]))
         gather_keys(0, 0)
         gather_keys(0, 1)
-        nc.sync.dma_start(gate_in[:], og.rearrange("b (j q) e -> q (b j) e", q=P))
         for h in range(2):
             cols = slice(h * T // 2, (h + 1) * T // 2)
             nc.scalar.activation(v_half[:, cols], v_pool[:, cols], ACT.Copy)
@@ -267,10 +262,11 @@ def tile_attend_soft_cap_gate_pgb2q256n512t2048_kernel(
         warm_up()
         vs_col = []
         for b in range(B):
-            vs_col.append(late.tile([P, PACK], F32, name="vs_col%d" % b, offset=HALF_AT + 64 * b, align_bytes=64))
+            vs_col.append(keep.tile([P, PACK], F32, name="vs_col%d" % b))
             nc.sync.dma_start(
-                vs_col[b][:], vs_row[0:1, b * N : (b + 1) * N].rearrange("o (p t) -> o p t", t=PACK)
+                vs_col[b][:], vs_row[VS_ROW:P, b * N : (b + 1) * N].rearrange("o (p t) -> o p t", t=PACK)
             )
+        nc.sync.dma_start(gate_in[:], og.rearrange("b (j q) e -> q (b j) e", q=P))
         for b in range(B):
             gather_keys(1, b)
             for j in range(QBLOCKS):

@@ -40,73 +40,83 @@ def tile_attend_soft_cap_gate_pgb2q256n512t2048_kernel(
         def list_of(b):
             return offsets[:, b * LIST_COLS : (b + 1) * LIST_COLS]
 
-        KW1_AT, Q0_AT, KS_AT, HALF_AT, VS_AT, LAST_AT = 0, 8192, 12288, 26624, 32768, 49152
+        ZERO_AT, KS_AT, HALF_AT, VS_AT, LAST_AT = 4032, 16384, 28672, 32768, 49152
+        KW0_AT = ZERO_AT + 64 + 4 * NQ
+        KW1_AT = KS_AT + T - 64
         DENSE = P - PASSES * 16
         VS_ROW = P - 1
         VS_GPSIMD = 1000
-        v_pool = keep.tile([P, T], F32, name="v_pool")
+        KS_SHIFT = (4, 0)
+        HALF = T // 2
         ks = keep.tile([P, PASSES, B * N], U8, name="ks", align_bytes=64)
-        zeros = late.tile([P, NQ // 4], I32, name="zeros", offset=Q0_AT - 128, align_bytes=64)
+        zeros = late.tile([P, NQ + 32], I32, name="zeros", offset=ZERO_AT, align_bytes=64)
         ident = keep.tile([P, P], F32, name="ident")
+        v_pool = [
+            keep.tile([P, HALF], F32, name="v_pool0"),
+            keep.tile([P, HALF], F32, name="v_pool1"),
+        ]
         kw_pool = [
-            keep.tile([P, T], U32, name="kw_pool0", align_bytes=64),
+            late.tile([P, T], U32, name="kw_pool0", offset=KW0_AT, align_bytes=64),
             late.tile([P, T], U32, name="kw_pool1", offset=KW1_AT, align_bytes=64),
         ]
         ks_pool = late.tile([P, T + 4], U8, name="ks_pool", offset=KS_AT, align_bytes=64)
         qs = keep.tile([P, NQ], U8, name="qs", align_bytes=64)
-        qw = [
-            late.tile([P, PASSES, NQ], U32, name="qw0", offset=Q0_AT, align_bytes=64),
-            late.tile([P, PASSES, NQ], U32, name="qw1", offset=KS_AT, align_bytes=64),
-        ]
+        qw00 = late.tile([P, NQ], U32, name="qw00", offset=ZERO_AT + 64, align_bytes=64)
+        qw01 = late.tile([P, NQ], U32, name="qw01", offset=KS_AT + 128, align_bytes=64)
+        qw1 = late.tile([P, PASSES, NQ], U32, name="qw1", offset=KS_AT + 64 - 8 * NQ, align_bytes=64)
+        qw = {(0, 0): qw00[:], (0, 1): qw01[:], (1, 0): qw1[:, 0], (1, 1): qw1[:, 1]}
         gate_in = late.tile([P, B * QBLOCKS, DV], F32, name="gate_in", offset=VS_AT, align_bytes=64)
         v_half = late.tile([P, T], BF16, name="v_half", offset=HALF_AT, align_bytes=64)
         vs_pool = late.tile([P, T + 1], F32, name="vs_pool", offset=VS_AT, align_bytes=64)
 
         nc.sync.dma_start(
-            ks_pool[DENSE:P, :T].bitcast(I32), k_scales.rearrange("o f t -> f o t").bitcast(I32)
+            ks_pool[DENSE:P, :T].bitcast(I32), k_scales.rearrange("o f t -> (o f) t").bitcast(I32)
         )
         nc.sync.dma_start(vs_pool[VS_ROW:P, :T], vs[0:1, :])
         for h in range(2):
-            cols = slice(h * T // 2, (h + 1) * T // 2)
-            nc.sync.dma_start(v_pool[:, cols], vT[:, cols])
+            nc.sync.dma_start(v_pool[h][:], vT[:, h * HALF : (h + 1) * HALF])
 
-        nc.gpsimd.memset(zeros[:], 0)
-        nc.gpsimd.tensor_copy(qs[:].bitcast(I32), zeros[:])
+        nc.gpsimd.memset(zeros[:, : NQ // 4], 0)
+        nc.gpsimd.tensor_copy(qs[:].bitcast(I32), zeros[:, : NQ // 4])
+        make_identity(nc, ident[:])
         nc.vector.memset(ks_pool[0:DENSE, :].bitcast(I32), 0)
         nc.gpsimd.memset(vs_pool[0:VS_ROW, :VS_GPSIMD].bitcast(I32), 0)
         nc.vector.memset(vs_pool[0:VS_ROW, VS_GPSIMD:].bitcast(I32), 0)
         nc.gpsimd.memset(ks[:].rearrange("p o n -> p (o n)").bitcast(I32), 0)
-        make_identity(nc, ident[:])
 
         def load_keys(o):
             nc.sync.dma_start(
                 kw_pool[o][:].bitcast(I32), k_words[o].rearrange("g t r -> g (t r)").bitcast(I32)
             )
 
-        def load_queries(b):
+        def load_first_queries(o):
             nc.sync.dma_start(
-                qw[b][:].bitcast(I32), q_words[b].rearrange("o g q r -> g o (q r)").bitcast(I32)
+                qw[0, o].bitcast(I32), q_words[0, o].rearrange("g q r -> g (q r)").bitcast(I32)
             )
 
-        load_keys(0)
         q_scale_rows = q_scales.rearrange("b o f n -> (b o) f n")
         for quad in range(4):
             nc.sync.dma_start(
                 qs[32 * quad : 32 * quad + 16, :].bitcast(I32),
                 q_scale_rows[:, 4 * quad : 4 * quad + 4, :].bitcast(I32),
             )
-        load_keys(1)
-        load_queries(0)
+        load_keys(0)
+        load_first_queries(0)
 
         ks_dense = keep.tile([P, B * N], U8, name="ks_dense", align_bytes=64)
         nc.vector.tensor_copy(ks_dense[:], ks_pool[:, :T].indirect(offsets[:]))
 
-        for quad in range(4):
-            nc.sync.dma_start(
-                ks[32 * quad : 32 * quad + 4].bitcast(I32),
-                ks_dense[DENSE + 8 * quad : DENSE + 8 * quad + 8, :].bitcast(I32),
-            )
-        load_queries(1)
+        def place_key_scales(o):
+            for quad in range(4):
+                src = DENSE + 16 * o + 4 * quad
+                dst = 32 * quad + KS_SHIFT[o]
+                nc.sync.dma_start(ks[dst : dst + 4, o].bitcast(I32), ks_dense[src : src + 4, :].bitcast(I32))
+
+        place_key_scales(0)
+        load_keys(1)
+        place_key_scales(1)
+        load_first_queries(1)
+        nc.sync.dma_start(qw1[:].bitcast(I32), q_words[1].rearrange("o g q r -> g o (q r)").bitcast(I32))
 
         kw = {}
 
@@ -115,13 +125,13 @@ def tile_attend_soft_cap_gate_pgb2q256n512t2048_kernel(
             nc.vector.tensor_copy(kw[o, b], kw_pool[o][:].indirect(list_of(b)))
 
         def warm_up():
-            idle = turn_ps.tile([P, N], F32, name="idle", tag="turn0")
+            idle = turn_ps.tile([P, N], F32, name="idle", tag="turn2")
             for first in (True, False):
                 nc.tensor.matmul_mx(
                     out=idle[:],
-                    lhsT=kw[0, 0][:, :P].bitcast(FP8X4),
+                    lhsT=kw_pool[0][:, :P].bitcast(FP8X4),
                     lhsT_scale=ks_dense[:, :P],
-                    rhs=kw[0, 0].bitcast(FP8X4),
+                    rhs=kw_pool[0][:, :N].bitcast(FP8X4),
                     rhs_scale=ks_dense[:, :N],
                     start=first,
                     stop=not first,
@@ -136,10 +146,10 @@ def tile_attend_soft_cap_gate_pgb2q256n512t2048_kernel(
             cols = slice(j * P, (j + 1) * P)
             nc.tensor.matmul_mx(
                 out=scores[b, j][:],
-                lhsT=qw[b][:, o, cols].bitcast(FP8X4),
+                lhsT=qw[b, o][:, cols].bitcast(FP8X4),
                 lhsT_scale=qs[4 * (b * PASSES + o) : P, cols],
                 rhs=kw[o, b].bitcast(FP8X4),
-                rhs_scale=ks[:, o, b * N : (b + 1) * N],
+                rhs_scale=ks[KS_SHIFT[o] : P, o, b * N : (b + 1) * N],
                 start=first,
                 stop=not first,
             )
@@ -176,42 +186,41 @@ def tile_attend_soft_cap_gate_pgb2q256n512t2048_kernel(
                 prob[i][:], neg_c[i][:], ACT.Exp, bias=neg_m[i][:], scale=-1.0, accum_out=total[:, i : i + 1]
             )
 
-        w_bf, w_codes, w_scales = {}, {}, {}
+        w_bf = keep.tile([P, B * QBLOCKS, P, PACK], BF16, name="w_bf", align_bytes=64)
+        w_codes = keep.tile([P, B * QBLOCKS, P], U32, name="w_codes", align_bytes=64)
+        w_scales = keep.tile([P, B * QBLOCKS, P], U8, name="w_scales", align_bytes=64)
 
         def weigh(i):
             b = blocks[i][0]
             bank = turn_ps.tile([P, PACK, P], F32, name="p_turned", tag="turn%d" % ((i + 2) % 4))
             for t in range(PACK):
                 nc.tensor.transpose(bank[:, t, :], prob[i][:, t * P : (t + 1) * P], ident[:])
-            w_bf[i] = keep.tile([P, P, PACK], BF16, name="w_bf%d" % i, align_bytes=64)
             nc.vector.tensor_tensor(
-                w_bf[i][:],
+                w_bf[:, i],
                 bank[:].rearrange("p t q -> p q t"),
                 vs_col[b][:].unsqueeze(1).to_broadcast([P, P, PACK]),
                 ALU.mult,
             )
 
-        def invert(b):
-            cols = slice(b * QBLOCKS, (b + 1) * QBLOCKS)
-            nc.vector.reciprocal(inv[:, cols], total[:, cols])
-
-        def quantise_w(i):
-            w_codes[i] = keep.tile([P, P], U32, name="w_codes%d" % i, align_bytes=64)
-            w_scales[i] = keep.tile([P, P], U8, name="w_scales%d" % i, align_bytes=64)
+        def quantise_w(first, last):
             nc.vector.quantize_mx(
-                out=w_codes[i][:].bitcast(FP8X4),
-                scales=w_scales[i][:],
-                in_=w_bf[i][:].rearrange("p q t -> p (q t)"),
+                out=w_codes[:, first:last].rearrange("p i q -> p (i q)").bitcast(FP8X4),
+                scales=w_scales[:, first:last].rearrange("p i q -> p (i q)"),
+                in_=w_bf[:, first:last].rearrange("p i q t -> p (i q t)"),
             )
 
         v_bf = keep.tile([P, B, DV, PACK], BF16, name="v_bf", align_bytes=64)
         v_codes = late.tile([P, B, DV], U32, name="v_codes", offset=KW1_AT, align_bytes=64)
         v_scales = keep.tile([P, B, DV], U8, name="v_scales", align_bytes=64)
 
+        picked = {}
+
+        def pick_values(b):
+            picked[b] = keep.tile([P, N], BF16, name="v_picked%d" % b)
+            nc.scalar.activation(picked[b][:], v_half[:].indirect(list_of(b)), ACT.Copy)
+
         def turn_values(b):
-            picked = keep.tile([P, N], BF16, name="v_picked%d" % b)
-            nc.scalar.activation(picked[:], v_half[:].indirect(list_of(b)), ACT.Copy)
-            words = picked[:].bitcast(F32)
+            words = picked[b][:].bitcast(F32)
             bank = turn_ps.tile([P, 2, DV], F32, name="v_turned", tag="turn%d" % b)[:]
             for u in range(2):
                 nc.tensor.transpose(bank[:, u, :], words[:, u : 2 * P : 2], ident[:])
@@ -239,8 +248,8 @@ def tile_attend_soft_cap_gate_pgb2q256n512t2048_kernel(
             y = score_ps.tile([P, DV], F32, name="y", tag="acc")
             nc.tensor.matmul_mx(
                 out=y[:],
-                lhsT=w_codes[i][:].bitcast(FP8X4),
-                lhsT_scale=w_scales[i][:],
+                lhsT=w_codes[:, i].bitcast(FP8X4),
+                lhsT_scale=w_scales[:, i],
                 rhs=v_codes[:, b, :].bitcast(FP8X4),
                 rhs_scale=v_scales[:, b, :],
                 start=True,
@@ -255,11 +264,14 @@ def tile_attend_soft_cap_gate_pgb2q256n512t2048_kernel(
         gather_keys(0, 0)
         gather_keys(0, 1)
         for h in range(2):
-            cols = slice(h * T // 2, (h + 1) * T // 2)
-            nc.scalar.activation(v_half[:, cols], v_pool[:, cols], ACT.Copy)
+            nc.scalar.activation(v_half[:, h * HALF : (h + 1) * HALF], v_pool[h][:], ACT.Copy)
+        pick_values(0)
         turn_values(0)
+        pick_values(1)
         turn_values(1)
         warm_up()
+        for j in range(QBLOCKS):
+            score_pass(0, 0, j, True)
         vs_col = []
         for b in range(B):
             vs_col.append(keep.tile([P, PACK], F32, name="vs_col%d" % b))
@@ -267,11 +279,13 @@ def tile_attend_soft_cap_gate_pgb2q256n512t2048_kernel(
                 vs_col[b][:], vs_row[VS_ROW:P, b * N : (b + 1) * N].rearrange("o (p t) -> o p t", t=PACK)
             )
         nc.sync.dma_start(gate_in[:], og.rearrange("b (j q) e -> q (b j) e", q=P))
-        for b in range(B):
-            gather_keys(1, b)
+        gather_keys(1, 0)
+        for j in range(QBLOCKS):
+            score_pass(1, 0, j, False)
+        gather_keys(1, 1)
+        for o in range(PASSES):
             for j in range(QBLOCKS):
-                score_pass(0, b, j, True)
-                score_pass(1, b, j, False)
+                score_pass(o, 1, j, o == 0)
         quantise_v()
         cap(0)
         row_max(0)
@@ -286,17 +300,13 @@ def tile_attend_soft_cap_gate_pgb2q256n512t2048_kernel(
         weigh(0)
         exponent(2)
         weigh(1)
-        quantise_w(0)
         exponent(3)
         make_gate()
-        invert(0)
         weigh(2)
-        quantise_w(1)
+        quantise_w(0, 2)
         weigh(3)
-        quantise_w(2)
-        invert(1)
-        finish(0)
-        quantise_w(3)
-        finish(1)
-        finish(2)
-        finish(3)
+        quantise_w(2, 3)
+        nc.vector.reciprocal(inv[:], total[:])
+        quantise_w(3, 4)
+        for i in range(B * QBLOCKS):
+            finish(i)

@@ -45,7 +45,7 @@ def tile_attend_soft_cap_gate_pgb2q256n512t2048_kernel(
         KW1_AT = KS_AT + T - 64
         DENSE = P - PASSES * 16
         VS_ROW = P - 1
-        VS_GPSIMD = 1000
+        VS_GPSIMD = 1304
         KS_SHIFT = (4, 0)
         HALF = T // 2
         ks = keep.tile([P, PASSES, B * N], U8, name="ks", align_bytes=64)
@@ -155,7 +155,7 @@ def tile_attend_soft_cap_gate_pgb2q256n512t2048_kernel(
             )
 
         capped, neg_c, neg_m, prob = {}, {}, {}, {}
-        total = keep.tile([P, B * QBLOCKS], F32, name="total")
+        total = keep.tile([P, B * QBLOCKS + 1], F32, name="total")
         inv = keep.tile([P, B * QBLOCKS], F32, name="inv")
 
         def cap(i):
@@ -180,11 +180,18 @@ def tile_attend_soft_cap_gate_pgb2q256n512t2048_kernel(
                 accum_out=neg_m[i][:],
             )
 
-        def exponent(i):
+        def exponent(i, parts=1):
             prob[i] = keep.tile([P, N], F32, name="prob%d" % i)
-            nc.scalar.activation(
-                prob[i][:], neg_c[i][:], ACT.Exp, bias=neg_m[i][:], scale=-1.0, accum_out=total[:, i : i + 1]
-            )
+            for h in range(parts):
+                cols = slice(h * N // parts, (h + 1) * N // parts)
+                nc.scalar.activation(
+                    prob[i][:, cols],
+                    neg_c[i][:, cols],
+                    ACT.Exp,
+                    bias=neg_m[i][:],
+                    scale=-1.0,
+                    accum_out=total[:, i + h : i + h + 1],
+                )
 
         w_bf = keep.tile([P, B * QBLOCKS, P, PACK], BF16, name="w_bf", align_bytes=64)
         w_codes = keep.tile([P, B * QBLOCKS, P], U32, name="w_codes", align_bytes=64)
@@ -283,30 +290,26 @@ def tile_attend_soft_cap_gate_pgb2q256n512t2048_kernel(
         for j in range(QBLOCKS):
             score_pass(1, 0, j, False)
         gather_keys(1, 1)
-        for o in range(PASSES):
-            for j in range(QBLOCKS):
+        for j in range(QBLOCKS):
+            for o in range(PASSES):
                 score_pass(o, 1, j, o == 0)
         quantise_v()
-        cap(0)
-        row_max(0)
-        cap(1)
-        row_max(1)
-        cap(2)
-        row_max(2)
+        for i in range(B * QBLOCKS):
+            cap(i)
+            row_max(i)
         exponent(0)
-        cap(3)
-        row_max(3)
         exponent(1)
-        weigh(0)
         exponent(2)
-        weigh(1)
-        exponent(3)
+        exponent(3, 2)
         make_gate()
-        weigh(2)
+        weigh(0)
+        weigh(1)
         quantise_w(0, 2)
+        weigh(2)
+        nc.vector.tensor_tensor(total[:, 3:4], total[:, 3:4], total[:, 4:5], ALU.add)
         weigh(3)
         quantise_w(2, 3)
-        nc.vector.reciprocal(inv[:], total[:])
+        nc.vector.reciprocal(inv[:], total[:, :4])
         quantise_w(3, 4)
         for i in range(B * QBLOCKS):
             finish(i)

@@ -16,6 +16,7 @@ U8 = mybir.dt.uint8
 FP8X4 = mybir.dt.float8_e4m3fn_x4
 ALU = mybir.AluOpType
 ACT = mybir.ActivationFunctionType
+AXIS = mybir.AxisListType
 
 P = 128
 PACK = 4
@@ -40,8 +41,8 @@ def tile_attend_soft_cap_gate_pgb2q256n512t2048_kernel(
         def list_of(b):
             return offsets[:, b * LIST_COLS : (b + 1) * LIST_COLS]
 
-        ZERO_AT, KS_AT, HALF_AT, VS_AT, LAST_AT = 4032, 16384, 28672, 32768, 49152
-        KW0_AT = ZERO_AT + 64 + 4 * NQ
+        Q00_AT, KS_AT, HALF_AT, VS_AT, LAST_AT, PROB_AT = 4096, 16384, 28672, 32768, 49152, 57344
+        KW0_AT = Q00_AT + 4 * NQ
         KW1_AT = KS_AT + T - 64
         DENSE = P - PASSES * 16
         VS_ROW = P - 1
@@ -49,7 +50,7 @@ def tile_attend_soft_cap_gate_pgb2q256n512t2048_kernel(
         KS_SHIFT = (4, 0)
         HALF = T // 2
         ks = keep.tile([P, PASSES, B * N], U8, name="ks", align_bytes=64)
-        zeros = late.tile([P, NQ + 32], I32, name="zeros", offset=ZERO_AT, align_bytes=64)
+        zeros = late.tile([P, NQ // 4], I32, name="zeros", offset=KW0_AT - 128, align_bytes=64)
         ident = keep.tile([P, P], F32, name="ident")
         v_pool = [
             keep.tile([P, HALF], F32, name="v_pool0"),
@@ -61,7 +62,7 @@ def tile_attend_soft_cap_gate_pgb2q256n512t2048_kernel(
         ]
         ks_pool = late.tile([P, T + 4], U8, name="ks_pool", offset=KS_AT, align_bytes=64)
         qs = keep.tile([P, NQ], U8, name="qs", align_bytes=64)
-        qw00 = late.tile([P, NQ], U32, name="qw00", offset=ZERO_AT + 64, align_bytes=64)
+        qw00 = late.tile([P, NQ], U32, name="qw00", offset=Q00_AT, align_bytes=64)
         qw01 = late.tile([P, NQ], U32, name="qw01", offset=KS_AT + 128, align_bytes=64)
         qw1 = late.tile([P, PASSES, NQ], U32, name="qw1", offset=KS_AT + 64 - 8 * NQ, align_bytes=64)
         qw = {(0, 0): qw00[:], (0, 1): qw01[:], (1, 0): qw1[:, 0], (1, 1): qw1[:, 1]}
@@ -76,8 +77,8 @@ def tile_attend_soft_cap_gate_pgb2q256n512t2048_kernel(
         for h in range(2):
             nc.sync.dma_start(v_pool[h][:], vT[:, h * HALF : (h + 1) * HALF])
 
-        nc.gpsimd.memset(zeros[:, : NQ // 4], 0)
-        nc.gpsimd.tensor_copy(qs[:].bitcast(I32), zeros[:, : NQ // 4])
+        nc.gpsimd.memset(zeros[:], 0)
+        nc.gpsimd.tensor_copy(qs[:].bitcast(I32), zeros[:])
         make_identity(nc, ident[:])
         nc.vector.memset(ks_pool[0:DENSE, :].bitcast(I32), 0)
         nc.gpsimd.memset(vs_pool[0:VS_ROW, :VS_GPSIMD].bitcast(I32), 0)
@@ -154,12 +155,14 @@ def tile_attend_soft_cap_gate_pgb2q256n512t2048_kernel(
                 stop=not first,
             )
 
-        capped, neg_c, neg_m, prob = {}, {}, {}, {}
+        capped, neg_m, prob = {}, {}, {}
         total = keep.tile([P, B * QBLOCKS + 1], F32, name="total")
         inv = keep.tile([P, B * QBLOCKS], F32, name="inv")
 
         def cap(i):
-            capped[i] = keep.tile([P, PACK, P], F32, name="capped%d" % i, align_bytes=64)
+            capped[i] = late.tile(
+                [P, PACK, P], F32, name="capped%d" % i, offset=LAST_AT + 2048 * (3 - i), align_bytes=64
+            )
             nc.scalar.activation(
                 capped[i][:],
                 scores[blocks[i]][:].rearrange("q (p t) -> q t p", t=PACK),
@@ -168,34 +171,28 @@ def tile_attend_soft_cap_gate_pgb2q256n512t2048_kernel(
             )
 
         def row_max(i):
-            neg_c[i] = late.tile([P, N], F32, name="neg_c%d" % i, offset=LAST_AT + 2048 * (3 - i), align_bytes=64)
-            neg_m[i] = keep.tile([P, 1], F32, name="neg_m%d" % i)
-            nc.vector.tensor_scalar(
-                neg_c[i][:],
-                capped[i][:].rearrange("q t p -> q (t p)"),
-                -CAP,
-                None,
-                ALU.mult,
-                ALU.min,
-                accum_out=neg_m[i][:],
+            neg_t = keep.tile([P, 1], F32, name="neg_t%d" % i)
+            nc.vector.tensor_reduce(
+                neg_t[:], capped[i][:].rearrange("q t p -> q (t p)"), axis=AXIS.X, op=ALU.max, negate=True
             )
+            neg_m[i] = keep.tile([P, 1], F32, name="neg_m%d" % i)
+            nc.gpsimd.tensor_scalar(neg_m[i][:], neg_t[:], CAP, 0.0, ALU.mult, ALU.add)
 
         def exponent(i, parts=1):
-            prob[i] = keep.tile([P, N], F32, name="prob%d" % i)
+            prob[i] = late.tile([P, N], F32, name="prob%d" % i, offset=PROB_AT + 2048 * i, align_bytes=64)
             for h in range(parts):
                 cols = slice(h * N // parts, (h + 1) * N // parts)
                 nc.scalar.activation(
                     prob[i][:, cols],
-                    neg_c[i][:, cols],
+                    capped[i][:].rearrange("q t p -> q (t p)")[:, cols],
                     ACT.Exp,
                     bias=neg_m[i][:],
-                    scale=-1.0,
+                    scale=CAP,
                     accum_out=total[:, i + h : i + h + 1],
                 )
 
         w_bf = keep.tile([P, B * QBLOCKS, P, PACK], BF16, name="w_bf", align_bytes=64)
-        w_codes = keep.tile([P, B * QBLOCKS, P], U32, name="w_codes", align_bytes=64)
-        w_scales = keep.tile([P, B * QBLOCKS, P], U8, name="w_scales", align_bytes=64)
+        w_codes, w_scales = {}, {}
 
         def weigh(i):
             b = blocks[i][0]
@@ -209,11 +206,13 @@ def tile_attend_soft_cap_gate_pgb2q256n512t2048_kernel(
                 ALU.mult,
             )
 
-        def quantise_w(first, last):
+        def quantise_w(i):
+            w_codes[i] = late.tile([P, P], U32, name="w_codes%d" % i, offset=PROB_AT + 2048 * (i + 1), align_bytes=64)
+            w_scales[i] = keep.tile([P, P], U8, name="w_scales%d" % i, align_bytes=64)
             nc.vector.quantize_mx(
-                out=w_codes[:, first:last].rearrange("p i q -> p (i q)").bitcast(FP8X4),
-                scales=w_scales[:, first:last].rearrange("p i q -> p (i q)"),
-                in_=w_bf[:, first:last].rearrange("p i q t -> p (i q t)"),
+                out=w_codes[i][:].bitcast(FP8X4),
+                scales=w_scales[i][:],
+                in_=w_bf[:, i].rearrange("p q t -> p (q t)"),
             )
 
         v_bf = keep.tile([P, B, DV, PACK], BF16, name="v_bf", align_bytes=64)
@@ -247,16 +246,19 @@ def tile_attend_soft_cap_gate_pgb2q256n512t2048_kernel(
         gate = keep.tile([P, B * QBLOCKS, DV], F32, name="gate")
 
         def make_gate():
-            nc.scalar.activation(gate_tanh[:], gate_in[:], ACT.Tanh, scale=0.5)
-            nc.scalar.activation(gate[:], gate_tanh[:], ACT.Copy, bias=0.5, scale=0.5)
+            halves = [slice(b * QBLOCKS, (b + 1) * QBLOCKS) for b in range(B)]
+            for half in halves:
+                nc.scalar.activation(gate_tanh[:, half], gate_in[:, half], ACT.Tanh, scale=0.5)
+            for half in halves:
+                nc.scalar.activation(gate[:, half], gate_tanh[:, half], ACT.Copy, bias=0.5, scale=0.5)
 
         def finish(i):
             b, j = blocks[i]
             y = score_ps.tile([P, DV], F32, name="y", tag="acc")
             nc.tensor.matmul_mx(
                 out=y[:],
-                lhsT=w_codes[:, i].bitcast(FP8X4),
-                lhsT_scale=w_scales[:, i],
+                lhsT=w_codes[i][:].bitcast(FP8X4),
+                lhsT_scale=w_scales[i][:],
                 rhs=v_codes[:, b, :].bitcast(FP8X4),
                 rhs_scale=v_scales[:, b, :],
                 start=True,
@@ -304,12 +306,13 @@ def tile_attend_soft_cap_gate_pgb2q256n512t2048_kernel(
         make_gate()
         weigh(0)
         weigh(1)
-        quantise_w(0, 2)
+        quantise_w(0)
         weigh(2)
-        nc.vector.tensor_tensor(total[:, 3:4], total[:, 3:4], total[:, 4:5], ALU.add)
+        quantise_w(1)
+        nc.gpsimd.tensor_tensor(total[:, 3:4], total[:, 3:4], total[:, 4:5], ALU.add)
         weigh(3)
-        quantise_w(2, 3)
+        quantise_w(2)
         nc.vector.reciprocal(inv[:], total[:, :4])
-        quantise_w(3, 4)
+        quantise_w(3)
         for i in range(B * QBLOCKS):
             finish(i)

@@ -41,48 +41,54 @@ def tile_attend_soft_cap_gate_pgb2q256n512t2048_kernel(
         def list_of(b):
             return offsets[:, b * LIST_COLS : (b + 1) * LIST_COLS]
 
-        Q00_AT, KS_AT, HALF_AT, VS_AT, LAST_AT, PROB_AT = 4096, 16384, 28672, 32768, 49152, 57344
+        Q00_AT, KS_AT, DENSE_AT, VS_AT, PICK_AT, LAST_AT, PROB_AT = 4096, 16384, 31744, 32768, 45056, 49152, 57344
+        KS_SPAN = 6144
         KW0_AT = Q00_AT + 4 * NQ
-        KW1_AT = KS_AT + T - 64
+        KW1_AT = KS_AT + KS_SPAN - 64
         DENSE = P - PASSES * 16
         VS_ROW = P - 1
-        VS_GPSIMD = 1304
+        VS_GPSIMD = 1000
         KS_SHIFT = (4, 0)
-        HALF = T // 2
+        ON_SCALAR = (256, 256)
         ks = keep.tile([P, PASSES, B * N], U8, name="ks", align_bytes=64)
         zeros = late.tile([P, NQ // 4], I32, name="zeros", offset=KW0_AT - 128, align_bytes=64)
         ident = keep.tile([P, P], F32, name="ident")
-        v_pool = [
-            keep.tile([P, HALF], F32, name="v_pool0"),
-            keep.tile([P, HALF], F32, name="v_pool1"),
-        ]
+        v_pool = keep.tile([P, T], F32, name="v_pool")
         kw_pool = [
             late.tile([P, T], U32, name="kw_pool0", offset=KW0_AT, align_bytes=64),
             late.tile([P, T], U32, name="kw_pool1", offset=KW1_AT, align_bytes=64),
         ]
-        ks_pool = late.tile([P, T + 4], U8, name="ks_pool", offset=KS_AT, align_bytes=64)
+        ks_pool = late.tile([P, KS_SPAN], U8, name="ks_pool", offset=KS_AT, align_bytes=64)
         qs = keep.tile([P, NQ], U8, name="qs", align_bytes=64)
-        qw00 = late.tile([P, NQ], U32, name="qw00", offset=Q00_AT, align_bytes=64)
-        qw01 = late.tile([P, NQ], U32, name="qw01", offset=KS_AT + 128, align_bytes=64)
-        qw1 = late.tile([P, PASSES, NQ], U32, name="qw1", offset=KS_AT + 64 - 8 * NQ, align_bytes=64)
-        qw = {(0, 0): qw00[:], (0, 1): qw01[:], (1, 0): qw1[:, 0], (1, 1): qw1[:, 1]}
-        gate_in = late.tile([P, B * QBLOCKS, DV], F32, name="gate_in", offset=VS_AT, align_bytes=64)
-        v_half = late.tile([P, T], BF16, name="v_half", offset=HALF_AT, align_bytes=64)
-        vs_pool = late.tile([P, T + 1], F32, name="vs_pool", offset=VS_AT, align_bytes=64)
+        q_at = {(0, 0): Q00_AT, (1, 0): KS_AT, (0, 1): KS_AT + 4 * NQ, (1, 1): KS_AT + 8 * NQ}
+        qw = {
+            key: late.tile([P, NQ], U32, name="qw%d%d" % key, offset=at, align_bytes=64)[:]
+            for key, at in q_at.items()
+        }
+        gate_in = late.tile([P, B * QBLOCKS, DV], F32, name="gate_in", offset=KS_AT + 12 * NQ, align_bytes=64)
+        vs_pool = late.tile([P, T], F32, name="vs_pool", offset=VS_AT, align_bytes=64)
+        naught = keep.tile([P, 1], F32, name="naught")
+        one_half = keep.tile([P, 1], F32, name="one_half")
 
         nc.sync.dma_start(
             ks_pool[DENSE:P, :T].bitcast(I32), k_scales.rearrange("o f t -> (o f) t").bitcast(I32)
         )
-        nc.sync.dma_start(vs_pool[VS_ROW:P, :T], vs[0:1, :])
-        for h in range(2):
-            nc.sync.dma_start(v_pool[h][:], vT[:, h * HALF : (h + 1) * HALF])
+        nc.sync.dma_start(v_pool[:], vT)
+        nc.sync.dma_start(vs_pool[VS_ROW:P, :], vs[0:1, :])
+
+        def clear(words):
+            last = words.shape[1] - 1
+            nc.vector.memset(words[:, :last], 0)
+            nc.vector.memset(words[:, last:], 0)
 
         nc.gpsimd.memset(zeros[:], 0)
         nc.gpsimd.tensor_copy(qs[:].bitcast(I32), zeros[:])
-        make_identity(nc, ident[:])
-        nc.vector.memset(ks_pool[0:DENSE, :].bitcast(I32), 0)
+        nc.vector.memset(naught[:], 0.0)
+        nc.scalar.activation(one_half[:], naught[:], ACT.Copy, bias=0.5)
+        clear(ks_pool[0:DENSE, :T].bitcast(I32))
         nc.gpsimd.memset(vs_pool[0:VS_ROW, :VS_GPSIMD].bitcast(I32), 0)
-        nc.vector.memset(vs_pool[0:VS_ROW, VS_GPSIMD:].bitcast(I32), 0)
+        clear(vs_pool[0:VS_ROW, VS_GPSIMD:].bitcast(I32))
+        make_identity(nc, ident[:])
         nc.gpsimd.memset(ks[:].rearrange("p o n -> p (o n)").bitcast(I32), 0)
 
         def load_keys(o):
@@ -90,9 +96,9 @@ def tile_attend_soft_cap_gate_pgb2q256n512t2048_kernel(
                 kw_pool[o][:].bitcast(I32), k_words[o].rearrange("g t r -> g (t r)").bitcast(I32)
             )
 
-        def load_first_queries(o):
+        def load_queries(b, o):
             nc.sync.dma_start(
-                qw[0, o].bitcast(I32), q_words[0, o].rearrange("g q r -> g (q r)").bitcast(I32)
+                qw[b, o].bitcast(I32), q_words[b, o].rearrange("g q r -> g (q r)").bitcast(I32)
             )
 
         q_scale_rows = q_scales.rearrange("b o f n -> (b o) f n")
@@ -102,9 +108,9 @@ def tile_attend_soft_cap_gate_pgb2q256n512t2048_kernel(
                 q_scale_rows[:, 4 * quad : 4 * quad + 4, :].bitcast(I32),
             )
         load_keys(0)
-        load_first_queries(0)
+        load_queries(0, 0)
 
-        ks_dense = keep.tile([P, B * N], U8, name="ks_dense", align_bytes=64)
+        ks_dense = late.tile([P, B * N], U8, name="ks_dense", offset=DENSE_AT, align_bytes=64)
         nc.vector.tensor_copy(ks_dense[:], ks_pool[:, :T].indirect(offsets[:]))
 
         def place_key_scales(o):
@@ -115,28 +121,17 @@ def tile_attend_soft_cap_gate_pgb2q256n512t2048_kernel(
 
         place_key_scales(0)
         load_keys(1)
+        load_queries(1, 0)
         place_key_scales(1)
-        load_first_queries(1)
-        nc.sync.dma_start(qw1[:].bitcast(I32), q_words[1].rearrange("o g q r -> g o (q r)").bitcast(I32))
+        load_queries(0, 1)
+        load_queries(1, 1)
+        nc.sync.dma_start(gate_in[:], og.rearrange("b (j q) e -> q (b j) e", q=P))
 
         kw = {}
 
         def gather_keys(o, b):
             kw[o, b] = keep.tile([P, N], U32, name="kw%d%d" % (o, b), align_bytes=64)[:]
             nc.vector.tensor_copy(kw[o, b], kw_pool[o][:].indirect(list_of(b)))
-
-        def warm_up():
-            idle = turn_ps.tile([P, N], F32, name="idle", tag="turn2")
-            for first in (True, False):
-                nc.tensor.matmul_mx(
-                    out=idle[:],
-                    lhsT=kw_pool[0][:, :P].bitcast(FP8X4),
-                    lhsT_scale=ks_dense[:, :P],
-                    rhs=kw_pool[0][:, :N].bitcast(FP8X4),
-                    rhs_scale=ks_dense[:, :N],
-                    start=first,
-                    stop=not first,
-                )
 
         blocks = [(b, j) for b in range(B) for j in range(QBLOCKS)]
         scores = {}
@@ -216,14 +211,17 @@ def tile_attend_soft_cap_gate_pgb2q256n512t2048_kernel(
             )
 
         v_bf = keep.tile([P, B, DV, PACK], BF16, name="v_bf", align_bytes=64)
-        v_codes = late.tile([P, B, DV], U32, name="v_codes", offset=KW1_AT, align_bytes=64)
+        v_codes = late.tile([P, B, DV], U32, name="v_codes", offset=KW1_AT + 1024, align_bytes=64)
         v_scales = keep.tile([P, B, DV], U8, name="v_scales", align_bytes=64)
-
-        picked = {}
+        picked = [
+            keep.tile([P, N], BF16, name="v_picked0"),
+            late.tile([P, N], BF16, name="v_picked1", offset=PICK_AT, align_bytes=64),
+        ]
 
         def pick_values(b):
-            picked[b] = keep.tile([P, N], BF16, name="v_picked%d" % b)
-            nc.scalar.activation(picked[b][:], v_half[:].indirect(list_of(b)), ACT.Copy)
+            cut = ON_SCALAR[b]
+            nc.scalar.activation(picked[b][:, :cut], v_pool[:].indirect(list_of(b)[:, : cut // 16]), ACT.Copy)
+            nc.vector.tensor_copy(picked[b][:, cut:], v_pool[:].indirect(list_of(b)[:, cut // 16 :]))
 
         def turn_values(b):
             words = picked[b][:].bitcast(F32)
@@ -242,13 +240,25 @@ def tile_attend_soft_cap_gate_pgb2q256n512t2048_kernel(
                 in_=v_bf[:].rearrange("p b e t -> p (b e t)"),
             )
 
+        vs_row = [
+            keep.tile([P, N], F32, name="vs_row0"),
+            late.tile([P, N], F32, name="vs_row1", offset=PICK_AT, align_bytes=64),
+        ]
+        vs_col = [
+            late.tile([P, PACK], F32, name="vs_col%d" % b, offset=DENSE_AT + 64 * b, align_bytes=64) for b in range(B)
+        ]
+
+        def pick_token_scales(b):
+            nc.scalar.activation(vs_row[b][:], vs_pool[:].indirect(list_of(b)), ACT.Copy)
+            nc.sync.dma_start(vs_col[b][:], vs_row[b][VS_ROW:P, :].rearrange("o (p t) -> o p t", t=PACK))
+
         gate_tanh = late.tile([P, B * QBLOCKS, DV], F32, name="gate_tanh", offset=LAST_AT, align_bytes=64)
         gate = keep.tile([P, B * QBLOCKS, DV], F32, name="gate")
 
         def make_gate():
             halves = [slice(b * QBLOCKS, (b + 1) * QBLOCKS) for b in range(B)]
             for half in halves:
-                nc.scalar.activation(gate_tanh[:, half], gate_in[:, half], ACT.Tanh, scale=0.5)
+                nc.scalar.activation(gate_tanh[:, half], gate_in[:, half], ACT.Tanh, scale=one_half[:])
             for half in halves:
                 nc.scalar.activation(gate[:, half], gate_tanh[:, half], ACT.Copy, bias=0.5, scale=0.5)
 
@@ -268,34 +278,21 @@ def tile_attend_soft_cap_gate_pgb2q256n512t2048_kernel(
             nc.vector.scalar_tensor_tensor(res[:], y[:], inv[:, i : i + 1], gate[:, i, :], ALU.mult, ALU.mult)
             nc.sync.dma_start(out[b, j * P : (j + 1) * P, :], res[:])
 
-        vs_row = keep.tile([P, B * N], F32, name="vs_row")
-        nc.vector.tensor_copy(vs_row[:], vs_pool[:, :T].indirect(offsets[:]))
+        pick_token_scales(0)
+        pick_values(0)
+        pick_values(1)
+        turn_values(0)
+        turn_values(1)
+        pick_token_scales(1)
         gather_keys(0, 0)
         gather_keys(0, 1)
-        for h in range(2):
-            nc.scalar.activation(v_half[:, h * HALF : (h + 1) * HALF], v_pool[h][:], ACT.Copy)
-        pick_values(0)
-        turn_values(0)
-        pick_values(1)
-        turn_values(1)
-        warm_up()
-        for j in range(QBLOCKS):
-            score_pass(0, 0, j, True)
-        vs_col = []
+        for b, j in blocks:
+            score_pass(0, b, j, True)
         for b in range(B):
-            vs_col.append(keep.tile([P, PACK], F32, name="vs_col%d" % b))
-            nc.sync.dma_start(
-                vs_col[b][:], vs_row[VS_ROW:P, b * N : (b + 1) * N].rearrange("o (p t) -> o p t", t=PACK)
-            )
-        nc.sync.dma_start(gate_in[:], og.rearrange("b (j q) e -> q (b j) e", q=P))
-        gather_keys(1, 0)
-        for j in range(QBLOCKS):
-            score_pass(1, 0, j, False)
-        gather_keys(1, 1)
-        for j in range(QBLOCKS):
-            for o in range(PASSES):
-                score_pass(o, 1, j, o == 0)
+            gather_keys(1, b)
         quantise_v()
+        for b, j in blocks:
+            score_pass(1, b, j, False)
         for i in range(B * QBLOCKS):
             cap(i)
             row_max(i)

@@ -70,11 +70,11 @@ def tile_attend_soft_cap_gate_pgb2q256n512t2048_kernel(
         naught = keep.tile([P, 1], F32, name="naught")
         one_half = keep.tile([P, 1], F32, name="one_half")
 
-        nc.sync.dma_start(
+        nc.scalar.dma_start(
             ks_pool[DENSE:P, :T].bitcast(I32), k_scales.rearrange("o f t -> (o f) t").bitcast(I32)
         )
         nc.sync.dma_start(v_pool[:], vT)
-        nc.sync.dma_start(vs_pool[VS_ROW:P, :], vs[0:1, :])
+        nc.scalar.dma_start(vs_pool[VS_ROW:P, :], vs[0:1, :])
 
         def clear(words):
             last = words.shape[1] - 1
@@ -114,7 +114,7 @@ def tile_attend_soft_cap_gate_pgb2q256n512t2048_kernel(
         nc.vector.tensor_copy(ks_dense[:], ks_pool[:, :T].indirect(offsets[:]))
 
         def place_key_scales(o):
-            for quad in range(4):
+            for quad in (0, 2, 1, 3):
                 src = DENSE + 16 * o + 4 * quad
                 dst = 32 * quad + KS_SHIFT[o]
                 nc.sync.dma_start(ks[dst : dst + 4, o].bitcast(I32), ks_dense[src : src + 4, :].bitcast(I32))

@@ -32,7 +32,7 @@ def tile_attend_soft_cap_gate_pgb2q256n512t2048_kernel(
     with ExitStack() as ctx:
         keep = ctx.enter_context(tc.tile_pool(name="keep", bufs=1))
         late = ctx.enter_context(tc.tile_pool(name="late", bufs=1))
-        score_ps = ctx.enter_context(tc.psum_pool(name="score_ps", bufs=4))
+        score_ps = ctx.enter_context(tc.psum_pool(name="score_ps", bufs=3))
         turn_ps = ctx.enter_context(tc.psum_pool(name="turn_ps", bufs=1))
 
         offsets = keep.tile([P, B * LIST_COLS], U16, name="offsets")
@@ -129,25 +129,28 @@ def tile_attend_soft_cap_gate_pgb2q256n512t2048_kernel(
 
         kw = {}
 
-        def gather_keys(o, b):
-            kw[o, b] = keep.tile([P, N], U32, name="kw%d%d" % (o, b), align_bytes=64)[:]
-            nc.vector.tensor_copy(kw[o, b], kw_pool[o][:].indirect(list_of(b)))
+        def gather_keys(o, b, slots=slice(0, N)):
+            if slots.start == 0:
+                kw[o, b] = keep.tile([P, N], U32, name="kw%d%d" % (o, b), align_bytes=64)[:]
+            entries = list_of(b)[:, slots.start // 16 : slots.stop // 16]
+            nc.vector.tensor_copy(kw[o, b][:, slots], kw_pool[o][:].indirect(entries))
 
         blocks = [(b, j) for b in range(B) for j in range(QBLOCKS)]
         scores = {}
 
-        def score_pass(o, b, j, first):
+        def score_pass(o, b, j, slots=slice(0, N)):
+            first = o == 0 and slots.start == 0
             if first:
                 scores[b, j] = score_ps.tile([P, N], F32, name="score", tag="acc")
             cols = slice(j * P, (j + 1) * P)
             nc.tensor.matmul_mx(
-                out=scores[b, j][:],
+                out=scores[b, j][:, slots],
                 lhsT=qw[b, o][:, cols].bitcast(FP8X4),
                 lhsT_scale=qs[4 * (b * PASSES + o) : P, cols],
-                rhs=kw[o, b].bitcast(FP8X4),
-                rhs_scale=ks[KS_SHIFT[o] : P, o, b * N : (b + 1) * N],
+                rhs=kw[o, b][:, slots].bitcast(FP8X4),
+                rhs_scale=ks[KS_SHIFT[o] : P, o, b * N + slots.start : b * N + slots.stop],
                 start=first,
-                stop=not first,
+                stop=o == PASSES - 1,
             )
 
         capped, neg_m, prob = {}, {}, {}
@@ -264,7 +267,10 @@ def tile_attend_soft_cap_gate_pgb2q256n512t2048_kernel(
 
         def finish(i):
             b, j = blocks[i]
-            y = score_ps.tile([P, DV], F32, name="y", tag="acc")
+            if i < 3:
+                y = score_ps.tile([P, DV], F32, name="y", tag="acc")
+            else:
+                y = turn_ps.tile([P, DV], F32, name="y_last")
             nc.tensor.matmul_mx(
                 out=y[:],
                 lhsT=w_codes[i][:].bitcast(FP8X4),
@@ -284,16 +290,19 @@ def tile_attend_soft_cap_gate_pgb2q256n512t2048_kernel(
         turn_values(0)
         turn_values(1)
         pick_token_scales(1)
-        gather_keys(0, 0)
+        for slots in (slice(0, N // 2), slice(N // 2, N)):
+            gather_keys(0, 0, slots)
+            for j in range(QBLOCKS):
+                score_pass(0, 0, j, slots)
         gather_keys(0, 1)
-        for b, j in blocks:
-            score_pass(0, b, j, True)
+        score_pass(0, 1, 0)
         for b in range(B):
             gather_keys(1, b)
         quantise_v()
-        for b, j in blocks:
-            score_pass(1, b, j, False)
-        for i in range(B * QBLOCKS):
+        for i, (b, j) in enumerate(blocks):
+            if i == 3:
+                score_pass(0, b, j)
+            score_pass(1, b, j)
             cap(i)
             row_max(i)
         exponent(0)

@@ -49,6 +49,7 @@ def tile_attend_soft_cap_gate_pgb2q256n512t2048_kernel(
         VS_ROW = P - 1
         VS_GPSIMD = 1000
         KS_SHIFT = (4, 0)
+        RUN = 4
         ON_SCALAR = (256, 256)
         ks = keep.tile([P, PASSES, B * N], U8, name="ks", align_bytes=64)
         zeros = late.tile([P, NQ // 4], I32, name="zeros", offset=KW0_AT - 128, align_bytes=64)
@@ -176,10 +177,10 @@ def tile_attend_soft_cap_gate_pgb2q256n512t2048_kernel(
             neg_m[i] = keep.tile([P, 1], F32, name="neg_m%d" % i)
             nc.gpsimd.tensor_scalar(neg_m[i][:], neg_t[:], CAP, 0.0, ALU.mult, ALU.add)
 
-        def exponent(i, parts=1):
+        def exponent(i, cuts=(0, N)):
             prob[i] = late.tile([P, N], F32, name="prob%d" % i, offset=PROB_AT + 2048 * i, align_bytes=64)
-            for h in range(parts):
-                cols = slice(h * N // parts, (h + 1) * N // parts)
+            for h in range(len(cuts) - 1):
+                cols = slice(cuts[h], cuts[h + 1])
                 nc.scalar.activation(
                     prob[i][:, cols],
                     capped[i][:].rearrange("q t p -> q (t p)")[:, cols],
@@ -198,9 +199,9 @@ def tile_attend_soft_cap_gate_pgb2q256n512t2048_kernel(
             for t in range(PACK):
                 nc.tensor.transpose(bank[:, t, :], prob[i][:, t * P : (t + 1) * P], ident[:])
             nc.vector.tensor_tensor(
-                w_bf[:, i],
-                bank[:].rearrange("p t q -> p q t"),
-                vs_col[b][:].unsqueeze(1).to_broadcast([P, P, PACK]),
+                w_bf[:, i].rearrange("p (c n) t -> p c t n", n=RUN),
+                bank[:].rearrange("p t (c n) -> p c t n", n=RUN),
+                vs_col[b][:].unsqueeze(1).unsqueeze(3).to_broadcast([P, P // RUN, PACK, RUN]),
                 ALU.mult,
             )
 
@@ -308,7 +309,7 @@ def tile_attend_soft_cap_gate_pgb2q256n512t2048_kernel(
         exponent(0)
         exponent(1)
         exponent(2)
-        exponent(3, 2)
+        exponent(3, (0, N - P, N))
         make_gate()
         weigh(0)
         weigh(1)

@@ -32,7 +32,7 @@ def tile_attend_soft_cap_gate_pgb2q256n512t2048_kernel(
     with ExitStack() as ctx:
         keep = ctx.enter_context(tc.tile_pool(name="keep", bufs=1))
         late = ctx.enter_context(tc.tile_pool(name="late", bufs=1))
-        score_ps = ctx.enter_context(tc.psum_pool(name="score_ps", bufs=3))
+        score_ps = ctx.enter_context(tc.psum_pool(name="score_ps", bufs=4))
         turn_ps = ctx.enter_context(tc.psum_pool(name="turn_ps", bufs=1))
 
         offsets = keep.tile([P, B * LIST_COLS], U16, name="offsets")
@@ -42,9 +42,10 @@ def tile_attend_soft_cap_gate_pgb2q256n512t2048_kernel(
             return offsets[:, b * LIST_COLS : (b + 1) * LIST_COLS]
 
         Q00_AT, KS_AT, DENSE_AT, VS_AT, PICK_AT, LAST_AT, PROB_AT = 4096, 16384, 31744, 32768, 45056, 49152, 57344
-        KS_SPAN = 6144
+        LATER = 5184
         KW0_AT = Q00_AT + 4 * NQ
-        KW1_AT = KS_AT + KS_SPAN - 64
+        KW1_AT = KS_AT + LATER - 64
+        prob_at = [KS_AT + 8 * NQ, KS_AT + 16 * NQ] + [PROB_AT + 2048 * i for i in range(3)]
         DENSE = P - PASSES * 16
         VS_ROW = P - 1
         VS_GPSIMD = 1000
@@ -53,20 +54,20 @@ def tile_attend_soft_cap_gate_pgb2q256n512t2048_kernel(
         ON_SCALAR = (256, 256)
         ks = keep.tile([P, PASSES, B * N], U8, name="ks", align_bytes=64)
         zeros = late.tile([P, NQ // 4], I32, name="zeros", offset=KW0_AT - 128, align_bytes=64)
+        more_zeros = late.tile([P, LATER // 4], I32, name="more_zeros", offset=KS_AT, align_bytes=64)
         ident = keep.tile([P, P], F32, name="ident")
         v_pool = keep.tile([P, T], F32, name="v_pool")
         kw_pool = [
             late.tile([P, T], U32, name="kw_pool0", offset=KW0_AT, align_bytes=64),
             late.tile([P, T], U32, name="kw_pool1", offset=KW1_AT, align_bytes=64),
         ]
-        ks_pool = late.tile([P, KS_SPAN], U8, name="ks_pool", offset=KS_AT, align_bytes=64)
+        ks_pool = keep.tile([P, T], U8, name="ks_pool", align_bytes=64)
         qs = keep.tile([P, NQ], U8, name="qs", align_bytes=64)
-        q_at = {(0, 0): Q00_AT, (1, 0): KS_AT, (0, 1): KS_AT + 4 * NQ, (1, 1): KS_AT + 8 * NQ}
-        qw = {
-            key: late.tile([P, NQ], U32, name="qw%d%d" % key, offset=at, align_bytes=64)[:]
-            for key, at in q_at.items()
-        }
-        gate_in = late.tile([P, B * QBLOCKS, DV], F32, name="gate_in", offset=KS_AT + 12 * NQ, align_bytes=64)
+        qw00 = late.tile([P, NQ], U32, name="qw00", offset=Q00_AT, align_bytes=64)
+        qw01 = late.tile([P, NQ], U32, name="qw01", offset=KS_AT + 8 * NQ, align_bytes=64)
+        qw1 = late.tile([P, PASSES, NQ], U32, name="qw1", offset=KS_AT + 12 * NQ, align_bytes=64)
+        qw = {(0, 0): qw00[:], (0, 1): qw01[:], (1, 0): qw1[:, 0], (1, 1): qw1[:, 1]}
+        gate_in = late.tile([P, B * QBLOCKS, DV], F32, name="gate_in", offset=KS_AT, align_bytes=64)
         vs_pool = late.tile([P, T], F32, name="vs_pool", offset=VS_AT, align_bytes=64)
         naught = keep.tile([P, 1], F32, name="naught")
         one_half = keep.tile([P, 1], F32, name="one_half")
@@ -90,7 +91,10 @@ def tile_attend_soft_cap_gate_pgb2q256n512t2048_kernel(
         nc.gpsimd.memset(vs_pool[0:VS_ROW, :VS_GPSIMD].bitcast(I32), 0)
         clear(vs_pool[0:VS_ROW, VS_GPSIMD:].bitcast(I32))
         make_identity(nc, ident[:])
-        nc.gpsimd.memset(ks[:].rearrange("p o n -> p (o n)").bitcast(I32), 0)
+        ks_words = ks[:].rearrange("p o n -> p (o n)").bitcast(I32).rearrange("p (r w) -> p r w", r=PASSES * B)
+        nc.gpsimd.memset(more_zeros[:, :32], 0)
+        nc.gpsimd.memset(ks_words[:, :, 8:], 0)
+        nc.gpsimd.tensor_copy(ks_words[:, :, :8], more_zeros[:, :32].rearrange("p (r w) -> p r w", w=8))
 
         def load_keys(o):
             nc.sync.dma_start(
@@ -112,20 +116,23 @@ def tile_attend_soft_cap_gate_pgb2q256n512t2048_kernel(
         load_queries(0, 0)
 
         ks_dense = late.tile([P, B * N], U8, name="ks_dense", offset=DENSE_AT, align_bytes=64)
-        nc.vector.tensor_copy(ks_dense[:], ks_pool[:, :T].indirect(offsets[:]))
+        for b in range(B):
+            nc.vector.tensor_copy(ks_dense[:, b * N : (b + 1) * N], ks_pool[:].indirect(list_of(b)))
 
-        def place_key_scales(o):
+        def place_key_scales(o, slots):
             for quad in (0, 2, 1, 3):
                 src = DENSE + 16 * o + 4 * quad
                 dst = 32 * quad + KS_SHIFT[o]
-                nc.sync.dma_start(ks[dst : dst + 4, o].bitcast(I32), ks_dense[src : src + 4, :].bitcast(I32))
+                nc.sync.dma_start(
+                    ks[dst : dst + 4, o, slots].bitcast(I32), ks_dense[src : src + 4, slots].bitcast(I32)
+                )
 
-        place_key_scales(0)
+        place_key_scales(0, slice(0, N))
         load_keys(1)
-        load_queries(1, 0)
-        place_key_scales(1)
+        place_key_scales(1, slice(0, B * N))
         load_queries(0, 1)
-        load_queries(1, 1)
+        nc.sync.dma_start(qw1[:].bitcast(I32), q_words[1].rearrange("o g q r -> g o (q r)").bitcast(I32))
+        place_key_scales(0, slice(N, B * N))
         nc.sync.dma_start(gate_in[:], og.rearrange("b (j q) e -> q (b j) e", q=P))
 
         kw = {}
@@ -155,7 +162,7 @@ def tile_attend_soft_cap_gate_pgb2q256n512t2048_kernel(
             )
 
         capped, neg_m, prob = {}, {}, {}
-        total = keep.tile([P, B * QBLOCKS + 1], F32, name="total")
+        total = keep.tile([P, B * QBLOCKS + 2], F32, name="total")
         inv = keep.tile([P, B * QBLOCKS], F32, name="inv")
 
         def cap(i):
@@ -178,16 +185,17 @@ def tile_attend_soft_cap_gate_pgb2q256n512t2048_kernel(
             nc.gpsimd.tensor_scalar(neg_m[i][:], neg_t[:], CAP, 0.0, ALU.mult, ALU.add)
 
         def exponent(i, cuts=(0, N)):
-            prob[i] = late.tile([P, N], F32, name="prob%d" % i, offset=PROB_AT + 2048 * i, align_bytes=64)
+            prob[i] = late.tile([P, N], F32, name="prob%d" % i, offset=prob_at[i], align_bytes=64)
             for h in range(len(cuts) - 1):
                 cols = slice(cuts[h], cuts[h + 1])
+                column = (i, 4 + i // 3)[h]
                 nc.scalar.activation(
                     prob[i][:, cols],
                     capped[i][:].rearrange("q t p -> q (t p)")[:, cols],
                     ACT.Exp,
                     bias=neg_m[i][:],
                     scale=CAP,
-                    accum_out=total[:, i + h : i + h + 1],
+                    accum_out=total[:, column : column + 1],
                 )
 
         w_bf = keep.tile([P, B * QBLOCKS, P, PACK], BF16, name="w_bf", align_bytes=64)
@@ -206,7 +214,7 @@ def tile_attend_soft_cap_gate_pgb2q256n512t2048_kernel(
             )
 
         def quantise_w(i):
-            w_codes[i] = late.tile([P, P], U32, name="w_codes%d" % i, offset=PROB_AT + 2048 * (i + 1), align_bytes=64)
+            w_codes[i] = late.tile([P, P], U32, name="w_codes%d" % i, offset=prob_at[i + 1], align_bytes=64)
             w_scales[i] = keep.tile([P, P], U8, name="w_scales%d" % i, align_bytes=64)
             nc.vector.quantize_mx(
                 out=w_codes[i][:].bitcast(FP8X4),
@@ -268,10 +276,7 @@ def tile_attend_soft_cap_gate_pgb2q256n512t2048_kernel(
 
         def finish(i):
             b, j = blocks[i]
-            if i < 3:
-                y = score_ps.tile([P, DV], F32, name="y", tag="acc")
-            else:
-                y = turn_ps.tile([P, DV], F32, name="y_last")
+            y = score_ps.tile([P, DV], F32, name="y", tag="acc")
             nc.tensor.matmul_mx(
                 out=y[:],
                 lhsT=w_codes[i][:].bitcast(FP8X4),
@@ -296,17 +301,16 @@ def tile_attend_soft_cap_gate_pgb2q256n512t2048_kernel(
             for j in range(QBLOCKS):
                 score_pass(0, 0, j, slots)
         gather_keys(0, 1)
-        score_pass(0, 1, 0)
         for b in range(B):
             gather_keys(1, b)
         quantise_v()
         for i, (b, j) in enumerate(blocks):
-            if i == 3:
+            if b == 1:
                 score_pass(0, b, j)
             score_pass(1, b, j)
             cap(i)
             row_max(i)
-        exponent(0)
+        exponent(0, (0, N - P, N))
         exponent(1)
         exponent(2)
         exponent(3, (0, N - P, N))
@@ -316,7 +320,7 @@ def tile_attend_soft_cap_gate_pgb2q256n512t2048_kernel(
         quantise_w(0)
         weigh(2)
         quantise_w(1)
-        nc.gpsimd.tensor_tensor(total[:, 3:4], total[:, 3:4], total[:, 4:5], ALU.add)
+        nc.gpsimd.tensor_tensor(total[:, 0:4:3], total[:, 0:4:3], total[:, 4:6], ALU.add)
         weigh(3)
         quantise_w(2)
         nc.vector.reciprocal(inv[:], total[:, :4])

@@ -162,7 +162,7 @@ def tile_attend_soft_cap_gate_pgb2q256n512t2048_kernel(
             )
 
         capped, neg_m, prob = {}, {}, {}
-        total = keep.tile([P, B * QBLOCKS + 2], F32, name="total")
+        total = keep.tile([P, 2 * B * QBLOCKS], F32, name="total")
         inv = keep.tile([P, B * QBLOCKS], F32, name="inv")
 
         def cap(i):
@@ -188,7 +188,7 @@ def tile_attend_soft_cap_gate_pgb2q256n512t2048_kernel(
             prob[i] = late.tile([P, N], F32, name="prob%d" % i, offset=prob_at[i], align_bytes=64)
             for h in range(len(cuts) - 1):
                 cols = slice(cuts[h], cuts[h + 1])
-                column = (i, 4 + i // 3)[h]
+                column = i + h * B * QBLOCKS
                 nc.scalar.activation(
                     prob[i][:, cols],
                     capped[i][:].rearrange("q t p -> q (t p)")[:, cols],
@@ -310,9 +310,9 @@ def tile_attend_soft_cap_gate_pgb2q256n512t2048_kernel(
             score_pass(1, b, j)
             cap(i)
             row_max(i)
-        exponent(0, (0, N - P, N))
-        exponent(1)
-        exponent(2)
+        exponent(0, (0, N // 2, N))
+        exponent(1, (0, N // 2, N))
+        exponent(2, (0, N // 2, N))
         exponent(3, (0, N - P, N))
         make_gate()
         weigh(0)
@@ -320,7 +320,7 @@ def tile_attend_soft_cap_gate_pgb2q256n512t2048_kernel(
         quantise_w(0)
         weigh(2)
         quantise_w(1)
-        nc.gpsimd.tensor_tensor(total[:, 0:4:3], total[:, 0:4:3], total[:, 4:6], ALU.add)
+        nc.gpsimd.tensor_tensor(total[:, :4], total[:, :4], total[:, 4:], ALU.add)
         weigh(3)
         quantise_w(2)
         nc.vector.reciprocal(inv[:], total[:, :4])

from contextlib import ExitStack

import concourse.mybir as mybir
from concourse.masks import make_identity

B, N, T, D, DV, NQ = 2, 512, 2048, 1024, 128, 256
CAP = 2.0
FLOPS = 2 * B * NQ * N * (D + DV)

F32 = mybir.dt.float32
BF16 = mybir.dt.bfloat16
I32 = mybir.dt.int32
U32 = mybir.dt.uint32
U16 = mybir.dt.uint16
U8 = mybir.dt.uint8
FP8X4 = mybir.dt.float8_e4m3fn_x4
ALU = mybir.AluOpType
ACT = mybir.ActivationFunctionType
AXIS = mybir.AxisListType

P = 128
PACK = 4
PASSES = D // (P * PACK)
QBLOCKS = NQ // P
LIST_COLS = N // 16


def tile_attend_soft_cap_gate_pgb2q256n512t2048_kernel(
    tc, q_words, q_scales, k_words, k_scales, vT, vs, og, offs, out
):
    nc = tc.nc
    with ExitStack() as ctx:
        keep = ctx.enter_context(tc.tile_pool(name="keep", bufs=1))
        late = ctx.enter_context(tc.tile_pool(name="late", bufs=1))
        score_ps = ctx.enter_context(tc.psum_pool(name="score_ps", bufs=4))
        turn_ps = ctx.enter_context(tc.psum_pool(name="turn_ps", bufs=1))

        offsets = keep.tile([P, B * LIST_COLS], U16, name="offsets")
        nc.sync.dma_start(offsets[:], offs)

        def list_of(b):
            return offsets[:, b * LIST_COLS : (b + 1) * LIST_COLS]

        Q00_AT, KS_AT, DENSE_AT, VS_AT, PICK_AT, LAST_AT, PROB_AT = 4096, 16384, 31744, 32768, 45056, 49152, 57344
        LATER = 5184
        KW0_AT = Q00_AT + 4 * NQ
        KW1_AT = KS_AT + LATER - 64
        prob_at = [KS_AT + 8 * NQ, KS_AT + 16 * NQ] + [PROB_AT + 2048 * i for i in range(3)]
        DENSE = P - PASSES * 16
        VS_ROW = P - 1
        VS_GPSIMD = 1000
        KS_SHIFT = (4, 0)
        RUN = 4
        ON_SCALAR = (256, 256)
        ks = keep.tile([P, PASSES, B * N], U8, name="ks", align_bytes=64)
        zeros = late.tile([P, NQ // 4], I32, name="zeros", offset=KW0_AT - 128, align_bytes=64)
        more_zeros = late.tile([P, LATER // 4], I32, name="more_zeros", offset=KS_AT, align_bytes=64)
        ident = keep.tile([P, P], F32, name="ident")
        v_pool = keep.tile([P, T], F32, name="v_pool")
        kw_pool = [
            late.tile([P, T], U32, name="kw_pool0", offset=KW0_AT, align_bytes=64),
            late.tile([P, T], U32, name="kw_pool1", offset=KW1_AT, align_bytes=64),
        ]
        ks_pool = keep.tile([P, T], U8, name="ks_pool", align_bytes=64)
        qs = keep.tile([P, NQ], U8, name="qs", align_bytes=64)
        qw00 = late.tile([P, NQ], U32, name="qw00", offset=Q00_AT, align_bytes=64)
        qw01 = late.tile([P, NQ], U32, name="qw01", offset=KS_AT + 8 * NQ, align_bytes=64)
        qw1 = late.tile([P, PASSES, NQ], U32, name="qw1", offset=KS_AT + 12 * NQ, align_bytes=64)
        qw = {(0, 0): qw00[:], (0, 1): qw01[:], (1, 0): qw1[:, 0], (1, 1): qw1[:, 1]}
        gate_in = late.tile([P, B * QBLOCKS, DV], F32, name="gate_in", offset=KS_AT, align_bytes=64)
        vs_pool = late.tile([P, T], F32, name="vs_pool", offset=VS_AT, align_bytes=64)
        naught = keep.tile([P, 1], F32, name="naught")
        one_half = keep.tile([P, 1], F32, name="one_half")

        nc.scalar.dma_start(
            ks_pool[DENSE:P, :T].bitcast(I32), k_scales.rearrange("o f t -> (o f) t").bitcast(I32)
        )
        nc.sync.dma_start(v_pool[:], vT)
        nc.scalar.dma_start(vs_pool[VS_ROW:P, :], vs[0:1, :])

        def clear(words):
            last = words.shape[1] - 1
            nc.vector.memset(words[:, :last], 0)
            nc.vector.memset(words[:, last:], 0)

        nc.gpsimd.memset(zeros[:], 0)
        nc.gpsimd.tensor_copy(qs[:].bitcast(I32), zeros[:])
        nc.vector.memset(naught[:], 0.0)
        nc.scalar.activation(one_half[:], naught[:], ACT.Copy, bias=0.5)
        clear(ks_pool[0:DENSE, :T].bitcast(I32))
        nc.gpsimd.memset(vs_pool[0:VS_ROW, :VS_GPSIMD].bitcast(I32), 0)
        clear(vs_pool[0:VS_ROW, VS_GPSIMD:].bitcast(I32))
        make_identity(nc, ident[:])
        ks_words = ks[:].rearrange("p o n -> p (o n)").bitcast(I32).rearrange("p (r w) -> p r w", r=PASSES * B)
        nc.gpsimd.memset(more_zeros[:, :32], 0)
        nc.gpsimd.memset(ks_words[:, :, 8:], 0)
        nc.gpsimd.tensor_copy(ks_words[:, :, :8], more_zeros[:, :32].rearrange("p (r w) -> p r w", w=8))

        def load_keys(o):
            nc.sync.dma_start(
                kw_pool[o][:].bitcast(I32), k_words[o].rearrange("g t r -> g (t r)").bitcast(I32)
            )

        def load_queries(b, o):
            nc.sync.dma_start(
                qw[b, o].bitcast(I32), q_words[b, o].rearrange("g q r -> g (q r)").bitcast(I32)
            )

        q_scale_rows = q_scales.rearrange("b o f n -> (b o) f n")
        for quad in range(4):
            nc.sync.dma_start(
                qs[32 * quad : 32 * quad + 16, :].bitcast(I32),
                q_scale_rows[:, 4 * quad : 4 * quad + 4, :].bitcast(I32),
            )
        load_keys(0)
        load_queries(0, 0)

        ks_dense = late.tile([P, B * N], U8, name="ks_dense", offset=DENSE_AT, align_bytes=64)
        for b in range(B):
            nc.vector.tensor_copy(ks_dense[:, b * N : (b + 1) * N], ks_pool[:].indirect(list_of(b)))

        def place_key_scales(o, slots):
            for quad in (0, 2, 1, 3):
                src = DENSE + 16 * o + 4 * quad
                dst = 32 * quad + KS_SHIFT[o]
                nc.sync.dma_start(
                    ks[dst : dst + 4, o, slots].bitcast(I32), ks_dense[src : src + 4, slots].bitcast(I32)
                )

        place_key_scales(0, slice(0, N))
        load_keys(1)
        place_key_scales(1, slice(0, B * N))
        load_queries(0, 1)
        nc.sync.dma_start(qw1[:].bitcast(I32), q_words[1].rearrange("o g q r -> g o (q r)").bitcast(I32))
        place_key_scales(0, slice(N, B * N))
        nc.sync.dma_start(gate_in[:], og.rearrange("b (j q) e -> q (b j) e", q=P))

        kw = {}

        def gather_keys(o, b, slots=slice(0, N)):
            if slots.start == 0:
                kw[o, b] = keep.tile([P, N], U32, name="kw%d%d" % (o, b), align_bytes=64)[:]
            entries = list_of(b)[:, slots.start // 16 : slots.stop // 16]
            nc.vector.tensor_copy(kw[o, b][:, slots], kw_pool[o][:].indirect(entries))

        blocks = [(b, j) for b in range(B) for j in range(QBLOCKS)]
        scores = {}

        def score_pass(o, b, j, slots=slice(0, N)):
            first = o == 0 and slots.start == 0
            if first:
                scores[b, j] = score_ps.tile([P, N], F32, name="score", tag="acc")
            cols = slice(j * P, (j + 1) * P)
            nc.tensor.matmul_mx(
                out=scores[b, j][:, slots],
                lhsT=qw[b, o][:, cols].bitcast(FP8X4),
                lhsT_scale=qs[4 * (b * PASSES + o) : P, cols],
                rhs=kw[o, b][:, slots].bitcast(FP8X4),
                rhs_scale=ks[KS_SHIFT[o] : P, o, b * N + slots.start : b * N + slots.stop],
                start=first,
                stop=o == PASSES - 1,
            )

        capped, neg_m, prob = {}, {}, {}
        total = keep.tile([P, 2 * B * QBLOCKS], F32, name="total")
        inv = keep.tile([P, B * QBLOCKS], F32, name="inv")

        def cap(i):
            capped[i] = late.tile(
                [P, PACK, P], F32, name="capped%d" % i, offset=LAST_AT + 2048 * (3 - i), align_bytes=64
            )
            nc.scalar.activation(
                capped[i][:],
                scores[blocks[i]][:].rearrange("q (p t) -> q t p", t=PACK),
                ACT.Tanh,
                scale=1.0 / CAP,
            )

        def row_max(i):
            neg_t = keep.tile([P, 1], F32, name="neg_t%d" % i)
            nc.vector.tensor_reduce(
                neg_t[:], capped[i][:].rearrange("q t p -> q (t p)"), axis=AXIS.X, op=ALU.max, negate=True
            )
            neg_m[i] = keep.tile([P, 1], F32, name="neg_m%d" % i)
            nc.gpsimd.tensor_scalar(neg_m[i][:], neg_t[:], CAP, 0.0, ALU.mult, ALU.add)

        def exponent(i, cuts=(0, N)):
            prob[i] = late.tile([P, N], F32, name="prob%d" % i, offset=prob_at[i], align_bytes=64)
            for h in range(len(cuts) - 1):
                cols = slice(cuts[h], cuts[h + 1])
                column = i + h * B * QBLOCKS
                nc.scalar.activation(
                    prob[i][:, cols],
                    capped[i][:].rearrange("q t p -> q (t p)")[:, cols],
                    ACT.Exp,
                    bias=neg_m[i][:],
                    scale=CAP,
                    accum_out=total[:, column : column + 1],
                )

        w_bf = keep.tile([P, B * QBLOCKS, P, PACK], BF16, name="w_bf", align_bytes=64)
        w_codes, w_scales = {}, {}

        def weigh(i):
            b = blocks[i][0]
            bank = turn_ps.tile([P, PACK, P], F32, name="p_turned", tag="turn%d" % ((i + 2) % 4))
            for t in range(PACK):
                nc.tensor.transpose(bank[:, t, :], prob[i][:, t * P : (t + 1) * P], ident[:])
            nc.vector.tensor_tensor(
                w_bf[:, i].rearrange("p (c n) t -> p c t n", n=RUN),
                bank[:].rearrange("p t (c n) -> p c t n", n=RUN),
                vs_col[b][:].unsqueeze(1).unsqueeze(3).to_broadcast([P, P // RUN, PACK, RUN]),
                ALU.mult,
            )

        def quantise_w(i):
            w_codes[i] = late.tile([P, P], U32, name="w_codes%d" % i, offset=prob_at[i + 1], align_bytes=64)
            w_scales[i] = keep.tile([P, P], U8, name="w_scales%d" % i, align_bytes=64)
            nc.vector.quantize_mx(
                out=w_codes[i][:].bitcast(FP8X4),
                scales=w_scales[i][:],
                in_=w_bf[:, i].rearrange("p q t -> p (q t)"),
            )

        v_bf = keep.tile([P, B, DV, PACK], BF16, name="v_bf", align_bytes=64)
        v_codes = late.tile([P, B, DV], U32, name="v_codes", offset=KW1_AT + 1024, align_bytes=64)
        v_scales = keep.tile([P, B, DV], U8, name="v_scales", align_bytes=64)
        picked = [
            keep.tile([P, N], BF16, name="v_picked0"),
            late.tile([P, N], BF16, name="v_picked1", offset=PICK_AT, align_bytes=64),
        ]

        def pick_values(b):
            cut = ON_SCALAR[b]
            nc.scalar.activation(picked[b][:, :cut], v_pool[:].indirect(list_of(b)[:, : cut // 16]), ACT.Copy)
            nc.vector.tensor_copy(picked[b][:, cut:], v_pool[:].indirect(list_of(b)[:, cut // 16 :]))

        def turn_values(b):
            words = picked[b][:].bitcast(F32)
            bank = turn_ps.tile([P, 2, DV], F32, name="v_turned", tag="turn%d" % b)[:]
            for u in range(2):
                nc.tensor.transpose(bank[:, u, :], words[:, u : 2 * P : 2], ident[:])
            nc.scalar.copy(
                v_bf[:, b].rearrange("p e t -> p (e t)").bitcast(F32).rearrange("p (e u) -> p e u", u=2),
                bank.rearrange("p u e -> p e u"),
            )

        def quantise_v():
            nc.vector.quantize_mx(
                out=v_codes[:].rearrange("p b e -> p (b e)").bitcast(FP8X4),
                scales=v_scales[:].rearrange("p b e -> p (b e)"),
                in_=v_bf[:].rearrange("p b e t -> p (b e t)"),
            )

        vs_row = [
            keep.tile([P, N], F32, name="vs_row0"),
            late.tile([P, N], F32, name="vs_row1", offset=PICK_AT, align_bytes=64),
        ]
        vs_col = [
            late.tile([P, PACK], F32, name="vs_col%d" % b, offset=DENSE_AT + 64 * b, align_bytes=64) for b in range(B)
        ]

        def pick_token_scales(b):
            nc.scalar.activation(vs_row[b][:], vs_pool[:].indirect(list_of(b)), ACT.Copy)
            nc.sync.dma_start(vs_col[b][:], vs_row[b][VS_ROW:P, :].rearrange("o (p t) -> o p t", t=PACK))

        gate_tanh = late.tile([P, B * QBLOCKS, DV], F32, name="gate_tanh", offset=LAST_AT, align_bytes=64)
        gate = keep.tile([P, B * QBLOCKS, DV], F32, name="gate")

        def make_gate():
            halves = [slice(b * QBLOCKS, (b + 1) * QBLOCKS) for b in range(B)]
            for half in halves:
                nc.scalar.activation(gate_tanh[:, half], gate_in[:, half], ACT.Tanh, scale=one_half[:])
            for half in halves:
                nc.scalar.activation(gate[:, half], gate_tanh[:, half], ACT.Copy, bias=0.5, scale=0.5)

        def finish(i):
            b, j = blocks[i]
            y = score_ps.tile([P, DV], F32, name="y", tag="acc")
            nc.tensor.matmul_mx(
                out=y[:],
                lhsT=w_codes[i][:].bitcast(FP8X4),
                lhsT_scale=w_scales[i][:],
                rhs=v_codes[:, b, :].bitcast(FP8X4),
                rhs_scale=v_scales[:, b, :],
                start=True,
                stop=True,
            )
            res = keep.tile([P, DV], F32, name="res%d" % i)
            nc.vector.scalar_tensor_tensor(res[:], y[:], inv[:, i : i + 1], gate[:, i, :], ALU.mult, ALU.mult)
            nc.sync.dma_start(out[b, j * P : (j + 1) * P, :], res[:])

        pick_token_scales(0)
        pick_values(0)
        pick_values(1)
        turn_values(0)
        turn_values(1)
        pick_token_scales(1)
        for slots in (slice(0, N // 2), slice(N // 2, N)):
            gather_keys(0, 0, slots)
            for j in range(QBLOCKS):
                score_pass(0, 0, j, slots)
        gather_keys(0, 1)
        for b in range(B):
            gather_keys(1, b)
        quantise_v()
        for i, (b, j) in enumerate(blocks):
            if b == 1:
                score_pass(0, b, j)
            score_pass(1, b, j)
            cap(i)
            row_max(i)
        exponent(0, (0, N // 2, N))
        exponent(1, (0, N // 2, N))
        exponent(2, (0, N // 2, N))
        exponent(3, (0, N - P, N))
        make_gate()
        weigh(0)
        weigh(1)
        quantise_w(0)
        weigh(2)
        quantise_w(1)
        nc.gpsimd.tensor_tensor(total[:, :4], total[:, :4], total[:, 4:], ALU.add)
        weigh(3)
        quantise_w(2)
        nc.vector.reciprocal(inv[:], total[:, :4])
        quantise_w(3)
        for i in range(B * QBLOCKS):
            finish(i)
